import numpy as np
import ml_dtypes


def mxq(x, axis, fmt="e4m3"):
    dtype, down = {"e4m3": (ml_dtypes.float8_e4m3fn, 7), "e5m2": (ml_dtypes.float8_e5m2, 14)}[fmt]
    v = np.moveaxis(np.asarray(x, np.float32).astype(ml_dtypes.bfloat16).astype(np.float64), axis, -1)
    blocks = v.reshape(v.shape[:-1] + (-1, 32))
    amax = np.abs(blocks).max(-1, keepdims=True)
    byte = np.maximum(np.where(amax > 0, np.frexp(amax)[1] - 1 + 127, 0) - down, 1)
    scale = np.exp2(byte - 127.0)
    codes = (blocks / scale).astype(np.float32).astype(dtype).astype(np.float64)
    return np.moveaxis((codes * scale).reshape(v.shape), -1, axis)


WIDE = False


def mx_kscale(k):
    if not WIDE:
        return np.ones(k)
    levels = np.array([10, -10, 5, -5, 0])
    if k % 512:
        return np.exp2(np.random.permutation(np.resize(levels, k // 32))).repeat(32)
    a = np.empty((k // 512, 16))
    for p in range(k // 512):
        a[p, :8] = np.random.permutation(np.resize(levels, 8))
        for g in range(8):
            far = levels[np.abs(levels - a[p, g]) >= 10]
            a[p, g + 8] = far[np.random.randint(len(far))]
    return np.exp2(a.ravel()).repeat(32)


def f64(x):
    return np.asarray(x).astype(np.float64)


def striped(idx):
    return np.tile(idx.reshape(-1, 16).T, (8, 1)).astype(np.uint16)


def unstriped(offs):
    return offs[:16].T.reshape(-1).astype(np.int64)


E2M1 = np.array([0.0, 0.5, 1.0, 1.5, 2.0, 3.0, 4.0, 6.0, -0.0, -0.5, -1.0, -1.5, -2.0, -3.0, -4.0, -6.0])


def pack_weight(w, fmt):
    k, n = w.shape
    w = f64(np.asarray(w, np.float32).astype(ml_dtypes.bfloat16)).reshape(k // 32, 32, n)
    amax = np.abs(w).max(1)
    if fmt == "e4m3":
        byte = np.frexp(amax)[1] - 1 + 127 - 7
    else:
        mant, ex = np.frexp(amax / 6.0)
        byte = np.where(mant > 0.5, ex, ex - 1) + 127
    byte = np.clip(np.where(amax > 0, byte, 1), 1, 254)
    scaled = (w * np.exp2(127.0 - byte)[:, None, :]).reshape(k, n).astype(np.float32)
    by_word = np.ascontiguousarray(scaled.reshape(k // 512, 128, 4, n).transpose(0, 1, 3, 2))
    if fmt == "e4m3":
        words = by_word.astype(ml_dtypes.float8_e4m3fn).view(np.uint8)
    else:
        c = by_word.astype(ml_dtypes.float4_e2m1fn).view(np.uint8) & 0xF
        words = (c[..., 0::2] | (c[..., 1::2] << 4)).reshape(k // 512, 128, 2 * n)
    return np.ascontiguousarray(words), np.ascontiguousarray(byte.astype(np.uint8).reshape(k // 512, 16, n))


def unpack_weight(words, scales, fmt):
    g, _, n = scales.shape
    words = np.ascontiguousarray(words).reshape(g, 128, n, -1)
    if fmt == "e4m3":
        vals = words.view(ml_dtypes.float8_e4m3fn).astype(np.float64)
    else:
        nib = np.empty((g, 128, n, 4), np.uint8)
        nib[..., 0::2] = words & 0xF
        nib[..., 1::2] = words >> 4
        vals = E2M1[nib]
    vals = vals * np.repeat(np.exp2(scales.astype(np.float64) - 127.0), 8, axis=1)[..., None]
    return vals.transpose(0, 1, 3, 2).reshape(g * 512, n)


def gelu(v):
    return 0.5 * v * (1.0 + np.tanh(np.sqrt(2.0 / np.pi) * (v + 0.044715 * v**3)))


K, K2, M, H, N, T, S, T2 = 512, 1024, 1024, 512, 512, 2048, 1024, 2048

def setup_inputs():
    n = np.random.standard_normal
    s = mx_kscale(K)[:, None]
    s2 = mx_kscale(K2)[:, None]
    u = mx_kscale(H)[:, None]
    tab_words, tab_scales = pack_weight(n((K, T)) * s, "e4m3")
    tab2_words, tab2_scales = pack_weight(n((K2, T)) * s2, "e4m3")
    wri_words, wri_scales = pack_weight(n((K, M)) / np.sqrt(K) / s, "e2m1")
    w4_words, w4_scales = pack_weight(n((H, N)) / np.sqrt(H) / u, "e4m3")
    perm = np.random.permutation(T2)
    return {
        "tab_words": tab_words, "tab_scales": tab_scales,
        "tab2_words": tab2_words, "tab2_scales": tab2_scales,
        "wri_words": wri_words, "wri_scales": wri_scales,
        "w3": (n((K2, H)) / np.sqrt(K2) / s2).astype(np.float32),
        "w4_words": w4_words, "w4_scales": w4_scales,
        "floor": np.random.uniform(0.1, 0.4, H).astype(np.float32),
        "scl": np.exp(0.5 * n((H, S))).astype(np.float32),
        "gain": (np.exp(0.3 * n(H)) * u[:, 0]).astype(np.float32),
        "wg1": np.exp(0.3 * n((128, S))).astype(np.float32),
        "wg2": np.exp(0.3 * n((128, S))).astype(np.float32),
        "offs": striped(np.random.permutation(T)[:S]),
        "offs2": striped(np.random.permutation(T)[:S]),
        "offs3": striped(perm[:S]), "offs4": striped(perm[S:])}

def reference(tab_words, tab_scales, tab2_words, tab2_scales, wri_words, wri_scales, w3, w4_words, w4_scales,
              floor, scl, gain, wg1, wg2, offs, offs2, offs3, offs4):
    v = unpack_weight(tab_words, tab_scales, "e4m3")[:, unstriped(offs)]
    v2 = unpack_weight(tab2_words, tab2_scales, "e4m3")[:, unstriped(offs2)]
    sq = np.square(unpack_weight(wri_words, wri_scales, "e2m1").T @ v)
    h1 = np.sqrt(sq[:H] + sq[H:] + f64(floor)[:, None])
    h2 = (mxq(f64(w3), 0, "e4m3").T @ v2) * f64(scl)
    page = np.zeros((H, T2))
    page[:, unstriped(offs3)] = np.tile(f64(wg1), (H // 128, 1)) * h1
    page[:, unstriped(offs4)] = np.tile(f64(wg2), (H // 128, 1)) * h2
    z = page * f64(gain)[:, None]
    return unpack_weight(w4_words, w4_scales, "e4m3").T @ mxq(z, 0, "e4m3")

@@ -1,0 +1,261 @@
+from contextlib import ExitStack
+
+import concourse.mybir as mybir
+from concourse.masks import make_identity
+
+K, K2, H, N, T, S = 512, 1024, 512, 512, 2048, 1024
+FLOPS = 2 * K * 2 * H * S + 2 * K2 * H * S + 2 * H * N * T
+
+F32 = mybir.dt.float32
+BF16 = mybir.dt.bfloat16
+I32 = mybir.dt.int32
+U32 = mybir.dt.uint32
+U16 = mybir.dt.uint16
+U8 = mybir.dt.uint8
+FP8X4 = mybir.dt.float8_e4m3fn_x4
+FP4X4 = mybir.dt.float4_e2m1fn_x4
+ACT = mybir.ActivationFunctionType
+MULT = mybir.AluOpType.mult
+
+P = 128
+PACK = 4
+BANK = 512
+HALF = S // 2
+LIST_COLS = S // 16
+WIDTHS = (128, 128, 256, 512, 512, 512)
+SCALAR_CHUNK = 5
+VECTOR_FROM = 8
+
+
+def tile_list_phonon_mode_weave_kernel(
+    tc, tab_words, tab_scales, tab2_words, tab2_scales, wri_words, wri_scales, w3, w4_words, w4_scales,
+    floor, scl, gain, wg1, wg2, offs, offs2, offs3, offs4, out,
+):
+    nc = tc.nc
+    with ExitStack() as ctx:
+        lists = ctx.enter_context(tc.tile_pool(name="lists", bufs=1))
+        keep = ctx.enter_context(tc.tile_pool(name="keep", bufs=1))
+        psum = ctx.enter_context(tc.psum_pool(name="psum", bufs=1))
+
+        def bank(b):
+            return psum.tile([P, BANK], F32, name="bank%d" % b)
+
+        def load_list(src, name):
+            t = lists.tile([P, LIST_COLS], U16, name=name)
+            nc.sync.dma_start(t[:], src)
+            return t
+
+        def scale_plane(engine, width, name):
+            t = keep.tile([P, width], U8, name=name, align_bytes=64)
+            engine.memset(t[:].bitcast(I32), 0)
+            return t
+
+        def load_scales(queue, plane, src):
+            rows = PACK * src.shape[0]
+            for q in range(4):
+                queue.dma_start(plane[:].bitcast(I32)[32 * q : 32 * q + rows, :], src[:, 4 * q : 4 * q + 4, :].bitcast(I32))
+
+        def load_words(src, width, name):
+            t = keep.tile([P, width], I32, name=name, align_bytes=64)
+            nc.sync.dma_start(t[:], src.rearrange("p t i -> p (t i)").bitcast(I32))
+            return t
+
+        def load_wg(src, i0, name):
+            t = keep.tile([P, 2, S], F32, name=name)
+            rows = src.rearrange("(q i) j -> q i j", i=PACK)[:, i0 : i0 + 2, :]
+            for q in (0, 2, 1, 3):
+                nc.sync.dma_start(t[32 * q : 32 * q + 32], rows)
+            return t
+
+        def load_channel_vector(src, name):
+            t = keep.tile([P, PACK], F32, name=name)
+            nc.sync.dma_start(t[:], src.rearrange("(p i) -> p i", i=PACK))
+            return t
+
+        tab_plane = scale_plane(nc.vector, T, "tab_plane")
+        wri_plane = scale_plane(nc.vector, 2 * H, "wri_plane")
+        tab2_plane = scale_plane(nc.gpsimd, T, "tab2_plane")
+        w4_plane = scale_plane(nc.gpsimd, N, "w4_plane")
+        ident = keep.tile([P, P], F32, name="ident")
+        make_identity(nc, ident[:])
+
+        list1 = load_list(offs, "list1")
+        list2 = load_list(offs2, "list2")
+        floor_t = load_channel_vector(floor, "floor_t")
+        load_scales(nc.sync, tab_plane, tab_scales)
+        tab_w = load_words(tab_words[0], T, "tab_w")
+        load_scales(nc.sync, wri_plane, wri_scales)
+        wri_w = keep.tile([P, 4 * H], U8, name="wri_w", align_bytes=64)
+        nc.sync.dma_start(wri_w[:].bitcast(I32), wri_words[0].bitcast(I32))
+        tab2_w = [load_words(tab2_words[a], T, "tab2_w%d" % a) for a in range(2)]
+        load_scales(nc.sync, tab2_plane, tab2_scales)
+        list3 = load_list(offs3, "list3")
+        wg1_t = [load_wg(wg1, 0, "wg1_lo")]
+        w3_raw = []
+        for a in range(2):
+            t = keep.tile([P, PACK, H], F32, name="w3_raw%d" % a)
+            nc.sync.dma_start(t[:], w3[512 * a : 512 * (a + 1), :].rearrange("(p j) c -> p j c", j=PACK))
+            w3_raw.append(t)
+        wg1_t.append(load_wg(wg1, 2, "wg1_hi"))
+        scl_t = []
+        for i in range(PACK):
+            t = keep.tile([P, S], F32, name="scl", tag="scl%d" % i)
+            nc.sync.dma_start(t[:], scl.rearrange("(p i) j -> p i j", i=PACK)[:, i, :])
+            scl_t.append(t)
+        gain_t = load_channel_vector(gain, "gain_t")
+        list4 = load_list(offs4, "list4")
+        wg2_t = [load_wg(wg2, 0, "wg2_lo"), load_wg(wg2, 2, "wg2_hi")]
+        w4_w = load_words(w4_words[0], N, "w4_w")
+        load_scales(nc.sync, w4_plane, w4_scales)
+
+        warm = keep.tile([P, 1], F32, name="warm")
+        nc.scalar.activation(warm[:], ident[:, 0:1], ACT.Sqrt)
+
+        v_scale = keep.tile([P, S], U8, name="v_scale", align_bytes=64)
+        nc.vector.tensor_copy(v_scale[:], tab_plane[:].indirect(list1[:]))
+        v_w = []
+        for h in range(2):
+            t = keep.tile([P, HALF], U32, name="v_w%d" % h, align_bytes=64)
+            nc.vector.tensor_copy(t[:], tab_w[:].bitcast(U32).indirect(list1[:, 32 * h : 32 * (h + 1)]))
+            v_w.append(t)
+        v2_w = []
+        for a in range(2):
+            t = keep.tile([P, S], U32, name="v2_w%d" % a, align_bytes=64)
+            nc.vector.tensor_copy(t[:], tab2_w[a][:].bitcast(U32).indirect(list2[:]))
+            v2_w.append(t)
+        v2_scale = keep.tile([P, S], U8, name="v2_scale", align_bytes=64)
+        nc.vector.tensor_copy(v2_scale[:], tab2_plane[:].indirect(list2[:]))
+
+        pages = [keep.tile([P, T], F32, name="page%d" % i) for i in range(PACK)]
+
+        squares = {}
+
+        def project(h):
+            for jb in range(4):
+                for part in range(2):
+                    acc = bank(2 * (jb % 2) + part)
+                    nc.tensor.matmul_mx(
+                        out=acc[:],
+                        lhsT=v_w[h][:, P * jb : P * (jb + 1)].bitcast(FP8X4),
+                        lhsT_scale=v_scale[:, HALF * h + P * jb : HALF * h + P * (jb + 1)],
+                        rhs=wri_w[:, 2 * H * part : 2 * H * (part + 1)].bitcast(FP4X4),
+                        rhs_scale=wri_plane[:, H * part : H * (part + 1)],
+                        start=True,
+                        stop=True,
+                    )
+                    sq = keep.tile([P, PACK, P], F32, name="sq", tag="bank_copy", bufs=16)
+                    nc.scalar.activation(sq[:], acc[:].rearrange("j (p i) -> j i p", i=PACK), ACT.Square)
+                    squares[(h, jb, part)] = sq
+
+        def sum_squares(i, h, b):
+            acc = bank(b)
+            for jb in range(4):
+                for part in range(2):
+                    nc.tensor.matmul(
+                        acc[:, P * jb : P * (jb + 1)], squares[(h, jb, part)][:, i, :], ident[:],
+                        start=(part == 0), stop=(part == 1), is_transpose=True,
+                    )
+            return acc
+
+        def stream1(i, h, b):
+            acc = sum_squares(i, h, b)
+            h1 = keep.tile([P, HALF], F32, name="h1_%d_%d" % (i, h))
+            nc.scalar.activation(h1[:], acc[:], ACT.Sqrt, bias=floor_t[:, i : i + 1])
+            nc.vector.tensor_tensor(
+                pages[i][:].indirect(list3[:, 32 * h : 32 * (h + 1)]), h1[:],
+                wg1_t[i // 2][:, i % 2, HALF * h : HALF * (h + 1)], MULT,
+            )
+
+        project(0)
+        stream1(0, 0, 4)
+        stream1(1, 0, 5)
+        project(1)
+        stream1(0, 1, 4)
+        stream1(1, 1, 5)
+
+        w3_w = []
+        w3_plane = []
+        for a in range(2):
+            grouped = keep.tile([P, PACK * H], BF16, name="w3_bf16_%d" % a, align_bytes=64)
+            nc.scalar.copy(
+                grouped[:].rearrange("p (i m j) -> p m j i", i=PACK, j=PACK),
+                w3_raw[a][:].rearrange("p j (m i) -> p m j i", i=PACK),
+            )
+            words = keep.tile([P, H], U32, name="w3_w%d" % a, align_bytes=64)
+            plane = keep.tile([P, H], U8, name="w3_plane%d" % a, align_bytes=64)
+            nc.vector.quantize_mx(out=words[:].bitcast(FP8X4), scales=plane[:], in_=grouped[:])
+            w3_w.append(words)
+            w3_plane.append(plane)
+
+        last = PACK - 1
+        stream1(2, 0, 0)
+        stream1(2, 1, 2)
+        last_sums = [sum_squares(last, h, 2 * h + 1) for h in range(2)]
+
+        z = keep.tile([P, T, PACK], BF16, name="z", align_bytes=64)
+
+        for i in range(PACK):
+            for h in range(2):
+                acc = bank((6, 7, 4, 5, 0, 2, 6, 7)[2 * i + h])
+                cols = slice(HALF * h, HALF * (h + 1))
+                for a in range(2):
+                    nc.tensor.matmul_mx(
+                        out=acc[:],
+                        lhsT=w3_w[a][:, P * i : P * (i + 1)].bitcast(FP8X4),
+                        lhsT_scale=w3_plane[a][:, P * i : P * (i + 1)],
+                        rhs=v2_w[a][:, cols].bitcast(FP8X4),
+                        rhs_scale=v2_scale[4 * a : P, cols],
+                        start=(a == 0),
+                        stop=(a == 1),
+                    )
+                nc.vector.tensor_tensor(scl_t[i][:, cols], acc[:], scl_t[i][:, cols], MULT)
+            nc.vector.tensor_tensor(pages[i][:].indirect(list4[:]), scl_t[i][:], wg2_t[i // 2][:, i % 2, :], MULT)
+            if i == last - 1:
+                h1_last = keep.tile([P, S], F32, name="h1_last", tag="scl%d" % i)
+                for h in range(2):
+                    nc.scalar.activation(
+                        h1_last[:, HALF * h : HALF * (h + 1)], last_sums[h][:], ACT.Sqrt, bias=floor_t[:, last : last + 1]
+                    )
+            if i < last:
+                gain_col = keep.tile([P, 1], F32, name="gain_col")
+                nc.scalar.copy(gain_col[:], gain_t[:, i : i + 1])
+                nc.scalar.activation(z[:, :, i], pages[i][:], ACT.Copy, scale=gain_col[:])
+
+        nc.vector.tensor_tensor(pages[last][:].indirect(list3[:]), h1_last[:], wg1_t[last // 2][:, last % 2, :], MULT)
+        gain_col = keep.tile([P, 1], F32, name="gain_col")
+        nc.scalar.copy(gain_col[:], gain_t[:, last : last + 1])
+        z_w = keep.tile([P, T], U32, name="z_w", align_bytes=64)
+        z_plane = keep.tile([P, T], U8, name="z_plane", align_bytes=64)
+        out_rows = out.rearrange("(m p) t -> p m t", p=P)
+        starts = [sum(WIDTHS[:c]) for c in range(len(WIDTHS))]
+        scalar_cols = slice(starts[SCALAR_CHUNK], starts[SCALAR_CHUNK] + WIDTHS[SCALAR_CHUNK])
+        nc.scalar.activation(z[:, scalar_cols, last], pages[last][:, scalar_cols], ACT.Copy, scale=gain_col[:])
+        filled = 0
+        for c, width in enumerate(WIDTHS):
+            cols = slice(starts[c], starts[c] + width)
+            if c != SCALAR_CHUNK:
+                nc.vector.tensor_scalar_mul(z[:, cols, last], pages[last][:, cols], gain_col[:])
+            nc.vector.quantize_mx(
+                out=z_w[:, cols].bitcast(FP8X4), scales=z_plane[:, cols], in_=z[:, cols, :].rearrange("p t i -> p (t i)")
+            )
+            groups = BANK // width
+            for m0 in range(0, N // P, groups):
+                acc = bank(filled % 8)
+                for g in range(groups):
+                    m = m0 + g
+                    nc.tensor.matmul_mx(
+                        out=acc[:, width * g : width * (g + 1)],
+                        lhsT=w4_w[:, P * m : P * (m + 1)].bitcast(FP8X4),
+                        lhsT_scale=w4_plane[:, P * m : P * (m + 1)],
+                        rhs=z_w[:, cols].bitcast(FP8X4),
+                        rhs_scale=z_plane[:, cols],
+                        start=True,
+                        stop=True,
+                    )
+                res = keep.tile([P, groups, width], F32, name="res", tag="bank_copy", bufs=16)
+                if filled >= VECTOR_FROM and filled % 2 == 0:
+                    nc.vector.tensor_copy(res[:].rearrange("p g t -> p (g t)"), acc[:])
+                else:
+                    nc.scalar.copy(res[:].rearrange("p g t -> p (g t)"), acc[:])
+                nc.sync.dma_start(out_rows[:, m0 : m0 + groups, cols], res[:])
+                filled = filled + 1

@@ -23,6 +23,7 @@ BANK = 512
 HALF = S // 2
 LIST_COLS = S // 16
 WIDTHS = (128, 128, 256, 512, 512, 512)
+UNITS = ((0, 256), (256, 512), (512, 1024))
 SCALAR_CHUNK = 5
 VECTOR_FROM = 8
 
@@ -51,21 +52,27 @@ def tile_list_phonon_mode_weave_kernel(
             return t
 
         def load_scales(queue, plane, src):
-            rows = PACK * src.shape[0]
-            for q in range(4):
-                queue.dma_start(plane[:].bitcast(I32)[32 * q : 32 * q + rows, :], src[:, 4 * q : 4 * q + 4, :].bitcast(I32))
+            for r in range(4):
+                queue.dma_start(plane[:].bitcast(I32)[r:P:32, :], src[0, r:16:4, :].bitcast(I32))
+
+        def load_scales_two_passes(plane, src):
+            for q in (0, 2, 1, 3):
+                nc.sync.dma_start(plane[:].bitcast(I32)[32 * q : 32 * q + 8, :], src[:, 4 * q : 4 * q + 4, :].bitcast(I32))
 
         def load_words(src, width, name):
             t = keep.tile([P, width], I32, name=name, align_bytes=64)
             nc.sync.dma_start(t[:], src.rearrange("p t i -> p (t i)").bitcast(I32))
             return t
 
-        def load_wg(src, i0, name):
-            t = keep.tile([P, 2, S], F32, name=name)
-            rows = src.rearrange("(q i) j -> q i j", i=PACK)[:, i0 : i0 + 2, :]
+        def load_wg(t, src, c0, c1):
+            rows = src.rearrange("(q i) j -> q (i j)", i=PACK)[:, c0:c1]
             for q in (0, 2, 1, 3):
-                nc.sync.dma_start(t[32 * q : 32 * q + 32], rows)
-            return t
+                nc.sync.dma_start(t[32 * q : 32 * q + 32, c0:c1], rows)
+
+        def load_wg1_low(t, j0, j1):
+            rows = wg1.rearrange("(q i) j -> q i j", i=PACK)[:, 0:2, j0:j1]
+            for q in (0, 2, 1, 3):
+                nc.sync.dma_start(t[:].rearrange("p (i j) -> p i j", i=PACK)[32 * q : 32 * q + 32, 0:2, j0:j1], rows)
 
         def load_channel_vector(src, name):
             t = keep.tile([P, PACK], F32, name=name)
@@ -87,24 +94,29 @@ def tile_list_phonon_mode_weave_kernel(
         load_scales(nc.sync, wri_plane, wri_scales)
         wri_w = keep.tile([P, 4 * H], U8, name="wri_w", align_bytes=64)
         nc.sync.dma_start(wri_w[:].bitcast(I32), wri_words[0].bitcast(I32))
-        tab2_w = [load_words(tab2_words[a], T, "tab2_w%d" % a) for a in range(2)]
-        load_scales(nc.sync, tab2_plane, tab2_scales)
+        load_scales_two_passes(tab2_plane, tab2_scales)
+        tab2_w = [load_words(tab2_words[0], T, "tab2_w0")]
         list3 = load_list(offs3, "list3")
-        wg1_t = [load_wg(wg1, 0, "wg1_lo")]
+        wg1_t = keep.tile([P, PACK * S], F32, name="wg1_t")
+        wg2_t = keep.tile([P, PACK * S], F32, name="wg2_t")
+        load_wg1_low(wg1_t, 0, HALF)
+        tab2_w.append(load_words(tab2_words[1], T, "tab2_w1"))
+        load_wg1_low(wg1_t, HALF, S)
+        load_wg(wg1_t, wg1, 2 * S, 2 * S + HALF)
         w3_raw = []
         for a in range(2):
             t = keep.tile([P, PACK, H], F32, name="w3_raw%d" % a)
             nc.sync.dma_start(t[:], w3[512 * a : 512 * (a + 1), :].rearrange("(p j) c -> p j c", j=PACK))
             w3_raw.append(t)
-        wg1_t.append(load_wg(wg1, 2, "wg1_hi"))
+        load_wg(wg1_t, wg1, 2 * S + HALF, PACK * S)
+        list4 = load_list(offs4, "list4")
+        gain_t = load_channel_vector(gain, "gain_t")
         scl_t = []
         for i in range(PACK):
-            t = keep.tile([P, S], F32, name="scl", tag="scl%d" % i)
+            t = keep.tile([P, S], F32, name="scl%d" % i)
             nc.sync.dma_start(t[:], scl.rearrange("(p i) j -> p i j", i=PACK)[:, i, :])
             scl_t.append(t)
-        gain_t = load_channel_vector(gain, "gain_t")
-        list4 = load_list(offs4, "list4")
-        wg2_t = [load_wg(wg2, 0, "wg2_lo"), load_wg(wg2, 2, "wg2_hi")]
+            load_wg(wg2_t, wg2, S * i, S * (i + 1))
         w4_w = load_words(w4_words[0], N, "w4_w")
         load_scales(nc.sync, w4_plane, w4_scales)
 
@@ -114,30 +126,29 @@ def tile_list_phonon_mode_weave_kernel(
         v_scale = keep.tile([P, S], U8, name="v_scale", align_bytes=64)
         nc.vector.tensor_copy(v_scale[:], tab_plane[:].indirect(list1[:]))
         v_w = []
-        for h in range(2):
-            t = keep.tile([P, HALF], U32, name="v_w%d" % h, align_bytes=64)
-            nc.vector.tensor_copy(t[:], tab_w[:].bitcast(U32).indirect(list1[:, 32 * h : 32 * (h + 1)]))
+        for j0, j1 in UNITS:
+            t = keep.tile([P, j1 - j0], U32, name="v_w%d" % j0, align_bytes=64)
+            nc.vector.tensor_copy(t[:], tab_w[:].bitcast(U32).indirect(list1[:, j0 // 16 : j1 // 16]))
             v_w.append(t)
-        v2_w = []
-        for a in range(2):
-            t = keep.tile([P, S], U32, name="v2_w%d" % a, align_bytes=64)
-            nc.vector.tensor_copy(t[:], tab2_w[a][:].bitcast(U32).indirect(list2[:]))
-            v2_w.append(t)
+        v2_w = [keep.tile([P, S], U32, name="v2_w%d" % a, align_bytes=64) for a in range(2)]
         v2_scale = keep.tile([P, S], U8, name="v2_scale", align_bytes=64)
         nc.vector.tensor_copy(v2_scale[:], tab2_plane[:].indirect(list2[:]))
+        nc.vector.tensor_copy(v2_w[0][:], tab2_w[0][:].bitcast(U32).indirect(list2[:]))
+        nc.vector.tensor_copy(v2_w[1][:], tab2_w[1][:].bitcast(U32).indirect(list2[:]))
 
         pages = [keep.tile([P, T], F32, name="page%d" % i) for i in range(PACK)]
 
         squares = {}
 
-        def project(h):
-            for jb in range(4):
+        def project(u, banks):
+            j0, j1 = UNITS[u]
+            for jb in range((j1 - j0) // P):
                 for part in range(2):
-                    acc = bank(2 * (jb % 2) + part)
+                    acc = bank(banks[2 * jb + part])
                     nc.tensor.matmul_mx(
                         out=acc[:],
-                        lhsT=v_w[h][:, P * jb : P * (jb + 1)].bitcast(FP8X4),
-                        lhsT_scale=v_scale[:, HALF * h + P * jb : HALF * h + P * (jb + 1)],
+                        lhsT=v_w[u][:, P * jb : P * (jb + 1)].bitcast(FP8X4),
+                        lhsT_scale=v_scale[:, j0 + P * jb : j0 + P * (jb + 1)],
                         rhs=wri_w[:, 2 * H * part : 2 * H * (part + 1)].bitcast(FP4X4),
                         rhs_scale=wri_plane[:, H * part : H * (part + 1)],
                         start=True,
@@ -145,41 +156,48 @@ def tile_list_phonon_mode_weave_kernel(
                     )
                     sq = keep.tile([P, PACK, P], F32, name="sq", tag="bank_copy", bufs=16)
                     nc.scalar.activation(sq[:], acc[:].rearrange("j (p i) -> j i p", i=PACK), ACT.Square)
-                    squares[(h, jb, part)] = sq
+                    squares[(j0 // P + jb, part)] = sq
 
-        def sum_squares(i, h, b):
+        def sum_squares(i, j0, j1, b):
             acc = bank(b)
-            for jb in range(4):
+            for jb in range((j1 - j0) // P):
                 for part in range(2):
                     nc.tensor.matmul(
-                        acc[:, P * jb : P * (jb + 1)], squares[(h, jb, part)][:, i, :], ident[:],
+                        acc[:, P * jb : P * (jb + 1)], squares[(j0 // P + jb, part)][:, i, :], ident[:],
                         start=(part == 0), stop=(part == 1), is_transpose=True,
                     )
-            return acc
+            return acc[:, 0 : j1 - j0]
 
-        def stream1(i, h, b):
-            acc = sum_squares(i, h, b)
-            h1 = keep.tile([P, HALF], F32, name="h1_%d_%d" % (i, h))
-            nc.scalar.activation(h1[:], acc[:], ACT.Sqrt, bias=floor_t[:, i : i + 1])
-            nc.vector.tensor_tensor(
-                pages[i][:].indirect(list3[:, 32 * h : 32 * (h + 1)]), h1[:],
-                wg1_t[i // 2][:, i % 2, HALF * h : HALF * (h + 1)], MULT,
-            )
+        def stream1_values(i, j0, j1, b):
+            sums = sum_squares(i, j0, j1, b)
+            h1 = keep.tile([P, j1 - j0], F32, name="h1_%d_%d" % (i, j0))
+            nc.scalar.activation(h1[:], sums, ACT.Sqrt, bias=floor_t[:, i : i + 1])
+            nc.gpsimd.tensor_tensor(h1[:], h1[:], wg1_t[:, S * i + j0 : S * i + j1], MULT)
+            return h1
 
-        project(0)
-        stream1(0, 0, 4)
-        stream1(1, 0, 5)
-        project(1)
-        stream1(0, 1, 4)
-        stream1(1, 1, 5)
+        def stream1_put(i, j0, j1, h1):
+            nc.vector.tensor_copy(pages[i][:].indirect(list3[:, j0 // 16 : j1 // 16]), h1[:])
 
+        def stream1(i, j0, j1, b):
+            stream1_put(i, j0, j1, stream1_values(i, j0, j1, b))
+
+        project(0, (0, 1, 2, 3))
+        stream1(0, *UNITS[0], 0)
+        stream1(1, *UNITS[0], 1)
+        project(1, (4, 5, 6, 7))
+        stream1(0, *UNITS[1], 4)
+        stream1(1, *UNITS[1], 5)
+        project(2, (2, 3, 6, 7, 0, 1, 4, 5))
+        stream1(0, *UNITS[2], 2)
+        stream1(1, *UNITS[2], 3)
+        stream1(2, 0, HALF, 6)
         w3_w = []
         w3_plane = []
         for a in range(2):
             grouped = keep.tile([P, PACK * H], BF16, name="w3_bf16_%d" % a, align_bytes=64)
             nc.scalar.copy(
-                grouped[:].rearrange("p (i m j) -> p m j i", i=PACK, j=PACK),
-                w3_raw[a][:].rearrange("p j (m i) -> p m j i", i=PACK),
+                grouped[:].rearrange("p (i m j) -> p m i j", i=PACK, j=PACK),
+                w3_raw[a][:].rearrange("p j (m i) -> p m i j", i=PACK),
             )
             words = keep.tile([P, H], U32, name="w3_w%d" % a, align_bytes=64)
             plane = keep.tile([P, H], U8, name="w3_plane%d" % a, align_bytes=64)
@@ -188,15 +206,16 @@ def tile_list_phonon_mode_weave_kernel(
             w3_plane.append(plane)
 
         last = PACK - 1
-        stream1(2, 0, 0)
-        stream1(2, 1, 2)
-        last_sums = [sum_squares(last, h, 2 * h + 1) for h in range(2)]
+        stream1(2, HALF, S, 7)
+        stream1(last, 0, HALF, 0)
+        h1_last = stream1_values(last, HALF, S, 1)
 
         z = keep.tile([P, T, PACK], BF16, name="z", align_bytes=64)
 
         for i in range(PACK):
+            nc.gpsimd.tensor_tensor(scl_t[i][:], scl_t[i][:], wg2_t[:, S * i : S * (i + 1)], MULT)
             for h in range(2):
-                acc = bank((6, 7, 4, 5, 0, 2, 6, 7)[2 * i + h])
+                acc = bank((2 + 2 * i + h) % 8)
                 cols = slice(HALF * h, HALF * (h + 1))
                 for a in range(2):
                     nc.tensor.matmul_mx(
@@ -208,20 +227,16 @@ def tile_list_phonon_mode_weave_kernel(
                         start=(a == 0),
                         stop=(a == 1),
                     )
-                nc.vector.tensor_tensor(scl_t[i][:, cols], acc[:], scl_t[i][:, cols], MULT)
-            nc.vector.tensor_tensor(pages[i][:].indirect(list4[:]), scl_t[i][:], wg2_t[i // 2][:, i % 2, :], MULT)
-            if i == last - 1:
-                h1_last = keep.tile([P, S], F32, name="h1_last", tag="scl%d" % i)
-                for h in range(2):
-                    nc.scalar.activation(
-                        h1_last[:, HALF * h : HALF * (h + 1)], last_sums[h][:], ACT.Sqrt, bias=floor_t[:, last : last + 1]
-                    )
+                h2 = keep.tile([P, BANK], F32, name="h2", tag="bank_copy", bufs=16)
+                nc.scalar.copy(h2[:], acc[:])
+                nc.gpsimd.tensor_tensor(scl_t[i][:, cols], scl_t[i][:, cols], h2[:], MULT)
+            nc.vector.tensor_copy(pages[i][:].indirect(list4[:]), scl_t[i][:])
             if i < last:
                 gain_col = keep.tile([P, 1], F32, name="gain_col")
                 nc.scalar.copy(gain_col[:], gain_t[:, i : i + 1])
                 nc.scalar.activation(z[:, :, i], pages[i][:], ACT.Copy, scale=gain_col[:])
 
-        nc.vector.tensor_tensor(pages[last][:].indirect(list3[:]), h1_last[:], wg1_t[last // 2][:, last % 2, :], MULT)
+        stream1_put(last, HALF, S, h1_last)
         gain_col = keep.tile([P, 1], F32, name="gain_col")
         nc.scalar.copy(gain_col[:], gain_t[:, last : last + 1])
         z_w = keep.tile([P, T], U32, name="z_w", align_bytes=64)

@@ -22,10 +22,8 @@ PACK = 4
 BANK = 512
 HALF = S // 2
 LIST_COLS = S // 16
-WIDTHS = (128, 128, 256, 512, 512, 512)
+WIDTHS = (256, 256, 512, 512, 512)
 UNITS = ((0, 256), (256, 512), (512, 1024))
-SCALAR_CHUNK = 5
-VECTOR_FROM = 8
 
 
 def tile_list_phonon_mode_weave_kernel(
@@ -99,24 +97,26 @@ def tile_list_phonon_mode_weave_kernel(
         list3 = load_list(offs3, "list3")
         wg1_t = keep.tile([P, PACK * S], F32, name="wg1_t")
         wg2_t = keep.tile([P, PACK * S], F32, name="wg2_t")
-        load_wg1_low(wg1_t, 0, HALF)
+        load_wg1_low(wg1_t, *UNITS[0])
+        load_wg1_low(wg1_t, *UNITS[1])
         tab2_w.append(load_words(tab2_words[1], T, "tab2_w1"))
-        load_wg1_low(wg1_t, HALF, S)
+        load_wg1_low(wg1_t, *UNITS[2])
         load_wg(wg1_t, wg1, 2 * S, 2 * S + HALF)
         w3_raw = []
         for a in range(2):
             t = keep.tile([P, PACK, H], F32, name="w3_raw%d" % a)
             nc.sync.dma_start(t[:], w3[512 * a : 512 * (a + 1), :].rearrange("(p j) c -> p j c", j=PACK))
             w3_raw.append(t)
-        load_wg(wg1_t, wg1, 2 * S + HALF, PACK * S)
+        load_wg(wg1_t, wg1, 2 * S + HALF, 3 * S + HALF)
         list4 = load_list(offs4, "list4")
         gain_t = load_channel_vector(gain, "gain_t")
         scl_t = []
         for i in range(PACK):
-            t = keep.tile([P, S], F32, name="scl%d" % i)
+            t = keep.tile([P, S], F32, name="scl", tag="row4k_%d" % i)
             nc.sync.dma_start(t[:], scl.rearrange("(p i) j -> p i j", i=PACK)[:, i, :])
             scl_t.append(t)
             load_wg(wg2_t, wg2, S * i, S * (i + 1))
+        load_wg(wg1_t, wg1, 3 * S + HALF, PACK * S)
         w4_w = load_words(w4_words[0], N, "w4_w")
         load_scales(nc.sync, w4_plane, w4_scales)
 
@@ -210,7 +210,9 @@ def tile_list_phonon_mode_weave_kernel(
         stream1(last, 0, HALF, 0)
         h1_last = stream1_values(last, HALF, S, 1)
 
-        z = keep.tile([P, T, PACK], BF16, name="z", align_bytes=64)
+        starts = [sum(WIDTHS[:c]) for c in range(len(WIDTHS))]
+        chunk_cols = [slice(starts[c], starts[c] + WIDTHS[c]) for c in range(len(WIDTHS))]
+        z = [keep.tile([P, width, PACK], BF16, name="z", tag="z%d" % c, align_bytes=64) for c, width in enumerate(WIDTHS)]
 
         for i in range(PACK):
             nc.gpsimd.tensor_tensor(scl_t[i][:], scl_t[i][:], wg2_t[:, S * i : S * (i + 1)], MULT)
@@ -234,7 +236,8 @@ def tile_list_phonon_mode_weave_kernel(
             if i < last:
                 gain_col = keep.tile([P, 1], F32, name="gain_col")
                 nc.scalar.copy(gain_col[:], gain_t[:, i : i + 1])
-                nc.scalar.activation(z[:, :, i], pages[i][:], ACT.Copy, scale=gain_col[:])
+                for c, cols in enumerate(chunk_cols):
+                    nc.scalar.activation(z[c][:, :, i], pages[i][:, cols], ACT.Copy, scale=gain_col[:])
 
         stream1_put(last, HALF, S, h1_last)
         gain_col = keep.tile([P, 1], F32, name="gain_col")
@@ -242,35 +245,61 @@ def tile_list_phonon_mode_weave_kernel(
         z_w = keep.tile([P, T], U32, name="z_w", align_bytes=64)
         z_plane = keep.tile([P, T], U8, name="z_plane", align_bytes=64)
         out_rows = out.rearrange("(m p) t -> p m t", p=P)
-        starts = [sum(WIDTHS[:c]) for c in range(len(WIDTHS))]
-        scalar_cols = slice(starts[SCALAR_CHUNK], starts[SCALAR_CHUNK] + WIDTHS[SCALAR_CHUNK])
-        nc.scalar.activation(z[:, scalar_cols, last], pages[last][:, scalar_cols], ACT.Copy, scale=gain_col[:])
-        filled = 0
-        for c, width in enumerate(WIDTHS):
-            cols = slice(starts[c], starts[c] + width)
-            if c != SCALAR_CHUNK:
-                nc.vector.tensor_scalar_mul(z[:, cols, last], pages[last][:, cols], gain_col[:])
+
+        def quantise(c):
+            cols = chunk_cols[c]
             nc.vector.quantize_mx(
-                out=z_w[:, cols].bitcast(FP8X4), scales=z_plane[:, cols], in_=z[:, cols, :].rearrange("p t i -> p (t i)")
+                out=z_w[:, cols].bitcast(FP8X4), scales=z_plane[:, cols], in_=z[c][:].rearrange("p t i -> p (t i)")
             )
+
+        def product(acc, m, c):
+            cols = chunk_cols[c]
+            nc.tensor.matmul_mx(
+                out=acc,
+                lhsT=w4_w[:, P * m : P * (m + 1)].bitcast(FP8X4),
+                lhsT_scale=w4_plane[:, P * m : P * (m + 1)],
+                rhs=z_w[:, cols].bitcast(FP8X4),
+                rhs_scale=z_plane[:, cols],
+                start=True,
+                stop=True,
+            )
+
+        def gain_after(c):
+            t = keep.tile([P, 1], F32, name="gain_late", tag="z%d" % c, align_bytes=64)
+            nc.gpsimd.tensor_copy(t[:], gain_t[:, last : last + 1])
+            return t
+
+        final = len(WIDTHS) - 1
+        nc.scalar.activation(z[final][:, :, last], pages[last][:, chunk_cols[final]], ACT.Copy, scale=gain_col[:])
+        filled = 0
+        for c in range(final - 1):
+            width = WIDTHS[c]
+            if c == 2:
+                gain_col = gain_after(0)
+            nc.vector.tensor_scalar_mul(z[c][:, :, last], pages[last][:, chunk_cols[c]], gain_col[:])
+            quantise(c)
             groups = BANK // width
             for m0 in range(0, N // P, groups):
-                acc = bank(filled % 8)
+                acc = bank(filled)
                 for g in range(groups):
-                    m = m0 + g
-                    nc.tensor.matmul_mx(
-                        out=acc[:, width * g : width * (g + 1)],
-                        lhsT=w4_w[:, P * m : P * (m + 1)].bitcast(FP8X4),
-                        lhsT_scale=w4_plane[:, P * m : P * (m + 1)],
-                        rhs=z_w[:, cols].bitcast(FP8X4),
-                        rhs_scale=z_plane[:, cols],
-                        start=True,
-                        stop=True,
-                    )
+                    product(acc[:, width * g : width * (g + 1)], m0 + g, c)
                 res = keep.tile([P, groups, width], F32, name="res", tag="bank_copy", bufs=16)
-                if filled >= VECTOR_FROM and filled % 2 == 0:
-                    nc.vector.tensor_copy(res[:].rearrange("p g t -> p (g t)"), acc[:])
-                else:
-                    nc.scalar.copy(res[:].rearrange("p g t -> p (g t)"), acc[:])
-                nc.sync.dma_start(out_rows[:, m0 : m0 + groups, cols], res[:])
+                nc.scalar.copy(res[:].rearrange("p g t -> p (g t)"), acc[:])
+                nc.sync.dma_start(out_rows[:, m0 : m0 + groups, chunk_cols[c]], res[:])
                 filled = filled + 1
+
+        nc.vector.tensor_scalar_mul(z[final - 1][:, :, last], pages[last][:, chunk_cols[final - 1]], gain_col[:])
+        quantise(final)
+        quantise(final - 1)
+        for m in range(N // P):
+            res = keep.tile([P, 2 * BANK], F32, name="res_pair", tag="row4k_%d" % m)
+            left = bank(2 * m)
+            product(left[:], m, final - 1)
+            nc.vector.tensor_copy(res[:, 0:BANK], left[:])
+            right = bank(2 * m + 1)
+            product(right[:], m, final)
+            if m == 0:
+                nc.vector.tensor_copy(res[:, BANK : 2 * BANK], right[:])
+            else:
+                nc.scalar.copy(res[:, BANK : 2 * BANK], right[:])
+            nc.sync.dma_start(out_rows[:, m, starts[final - 1] : T], res[:])

@@ -77,7 +77,9 @@ def tile_list_phonon_mode_weave_kernel(
             nc.sync.dma_start(t[:], src.rearrange("(p i) -> p i", i=PACK))
             return t
 
-        tab_plane = scale_plane(nc.vector, T, "tab_plane")
+        tab_plane = keep.tile([P, T], U8, name="tab_plane", align_bytes=64)
+        nc.vector.memset(tab_plane[:, 0:S].bitcast(I32), 0)
+        nc.gpsimd.memset(tab_plane[:, S:T].bitcast(I32), 0)
         wri_plane = scale_plane(nc.vector, 2 * H, "wri_plane")
         tab2_plane = scale_plane(nc.gpsimd, T, "tab2_plane")
         w4_plane = scale_plane(nc.gpsimd, N, "w4_plane")
@@ -86,13 +88,13 @@ def tile_list_phonon_mode_weave_kernel(
 
         list1 = load_list(offs, "list1")
         list2 = load_list(offs2, "list2")
-        floor_t = load_channel_vector(floor, "floor_t")
         load_scales(nc.sync, tab_plane, tab_scales)
         tab_w = load_words(tab_words[0], T, "tab_w")
         load_scales(nc.sync, wri_plane, wri_scales)
         wri_w = keep.tile([P, 4 * H], U8, name="wri_w", align_bytes=64)
         nc.sync.dma_start(wri_w[:].bitcast(I32), wri_words[0].bitcast(I32))
         load_scales_two_passes(tab2_plane, tab2_scales)
+        floor_t = load_channel_vector(floor, "floor_t")
         tab2_w = [load_words(tab2_words[0], T, "tab2_w0")]
         list3 = load_list(offs3, "list3")
         wg1_t = keep.tile([P, PACK * S], F32, name="wg1_t")
@@ -107,7 +109,8 @@ def tile_list_phonon_mode_weave_kernel(
             t = keep.tile([P, PACK, H], F32, name="w3_raw%d" % a)
             nc.sync.dma_start(t[:], w3[512 * a : 512 * (a + 1), :].rearrange("(p j) c -> p j c", j=PACK))
             w3_raw.append(t)
-        load_wg(wg1_t, wg1, 2 * S + HALF, 3 * S + HALF)
+        load_wg(wg1_t, wg1, 2 * S + HALF, 3 * S)
+        load_wg(wg1_t, wg1, 3 * S, 3 * S + HALF)
         list4 = load_list(offs4, "list4")
         gain_t = load_channel_vector(gain, "gain_t")
         scl_t = []
@@ -168,12 +171,13 @@ def tile_list_phonon_mode_weave_kernel(
                     )
             return acc[:, 0 : j1 - j0]
 
-        def stream1_values(i, j0, j1, b):
+        def stream1_values(i, j0, j1, b, weighted=None):
             sums = sum_squares(i, j0, j1, b)
             h1 = keep.tile([P, j1 - j0], F32, name="h1_%d_%d" % (i, j0))
             nc.scalar.activation(h1[:], sums, ACT.Sqrt, bias=floor_t[:, i : i + 1])
-            nc.gpsimd.tensor_tensor(h1[:], h1[:], wg1_t[:, S * i + j0 : S * i + j1], MULT)
-            return h1
+            weighted = h1 if weighted is None else weighted
+            nc.gpsimd.tensor_tensor(weighted[:], h1[:], wg1_t[:, S * i + j0 : S * i + j1], MULT)
+            return weighted
 
         def stream1_put(i, j0, j1, h1):
             nc.vector.tensor_copy(pages[i][:].indirect(list3[:, j0 // 16 : j1 // 16]), h1[:])
@@ -191,23 +195,20 @@ def tile_list_phonon_mode_weave_kernel(
         stream1(0, *UNITS[2], 2)
         stream1(1, *UNITS[2], 3)
         stream1(2, 0, HALF, 6)
-        w3_w = []
-        w3_plane = []
+        grouped = keep.tile([P, 2, PACK * H], BF16, name="w3_bf16", tag="w3_bf16", align_bytes=64)
         for a in range(2):
-            grouped = keep.tile([P, PACK * H], BF16, name="w3_bf16_%d" % a, align_bytes=64)
             nc.scalar.copy(
-                grouped[:].rearrange("p (i m j) -> p m i j", i=PACK, j=PACK),
+                grouped[:, a, :].rearrange("p (i m j) -> p m i j", i=PACK, j=PACK),
                 w3_raw[a][:].rearrange("p j (m i) -> p m i j", i=PACK),
             )
-            words = keep.tile([P, H], U32, name="w3_w%d" % a, align_bytes=64)
-            plane = keep.tile([P, H], U8, name="w3_plane%d" % a, align_bytes=64)
-            nc.vector.quantize_mx(out=words[:].bitcast(FP8X4), scales=plane[:], in_=grouped[:])
-            w3_w.append(words)
-            w3_plane.append(plane)
+        w3_w = keep.tile([P, 2 * H], U32, name="w3_w", align_bytes=64)
+        w3_plane = keep.tile([P, 2 * H], U8, name="w3_plane", align_bytes=64)
+        nc.vector.quantize_mx(out=w3_w[:].bitcast(FP8X4), scales=w3_plane[:], in_=grouped[:].rearrange("p a c -> p (a c)"))
 
         last = PACK - 1
         stream1(2, HALF, S, 7)
-        stream1(last, 0, HALF, 0)
+        after_w3 = keep.tile([P, HALF], F32, name="after_w3", tag="w3_bf16", align_bytes=64)
+        stream1_put(last, 0, HALF, stream1_values(last, 0, HALF, 0, after_w3))
         h1_last = stream1_values(last, HALF, S, 1)
 
         starts = [sum(WIDTHS[:c]) for c in range(len(WIDTHS))]
@@ -222,8 +223,8 @@ def tile_list_phonon_mode_weave_kernel(
                 for a in range(2):
                     nc.tensor.matmul_mx(
                         out=acc[:],
-                        lhsT=w3_w[a][:, P * i : P * (i + 1)].bitcast(FP8X4),
-                        lhsT_scale=w3_plane[a][:, P * i : P * (i + 1)],
+                        lhsT=w3_w[:, H * a + P * i : H * a + P * (i + 1)].bitcast(FP8X4),
+                        lhsT_scale=w3_plane[:, H * a + P * i : H * a + P * (i + 1)],
                         rhs=v2_w[a][:, cols].bitcast(FP8X4),
                         rhs_scale=v2_scale[4 * a : P, cols],
                         start=(a == 0),

@@ -67,10 +67,10 @@ def tile_list_phonon_mode_weave_kernel(
             for q in (0, 2, 1, 3):
                 nc.sync.dma_start(t[32 * q : 32 * q + 32, c0:c1], rows)
 
-        def load_wg1_low(t, j0, j1):
-            rows = wg1.rearrange("(q i) j -> q i j", i=PACK)[:, 0:2, j0:j1]
+        def load_wg1(t, i0, i1, j0, j1):
+            rows = wg1.rearrange("(q i) j -> q i j", i=PACK)[:, i0:i1, j0:j1]
             for q in (0, 2, 1, 3):
-                nc.sync.dma_start(t[:].rearrange("p (i j) -> p i j", i=PACK)[32 * q : 32 * q + 32, 0:2, j0:j1], rows)
+                nc.sync.dma_start(t[:].rearrange("p (i j) -> p i j", i=PACK)[32 * q : 32 * q + 32, i0:i1, j0:j1], rows)
 
         def load_channel_vector(src, name):
             t = keep.tile([P, PACK], F32, name=name)
@@ -99,18 +99,16 @@ def tile_list_phonon_mode_weave_kernel(
         list3 = load_list(offs3, "list3")
         wg1_t = keep.tile([P, PACK * S], F32, name="wg1_t")
         wg2_t = keep.tile([P, PACK * S], F32, name="wg2_t")
-        load_wg1_low(wg1_t, *UNITS[0])
-        load_wg1_low(wg1_t, *UNITS[1])
         tab2_w.append(load_words(tab2_words[1], T, "tab2_w1"))
-        load_wg1_low(wg1_t, *UNITS[2])
-        load_wg(wg1_t, wg1, 2 * S, 2 * S + HALF)
+        load_wg1(wg1_t, 0, 2, *UNITS[0])
+        load_wg1(wg1_t, 2, 4, *UNITS[0])
+        load_wg1(wg1_t, 0, 4, *UNITS[1])
         w3_raw = []
         for a in range(2):
             t = keep.tile([P, PACK, H], F32, name="w3_raw%d" % a)
             nc.sync.dma_start(t[:], w3[512 * a : 512 * (a + 1), :].rearrange("(p j) c -> p j c", j=PACK))
             w3_raw.append(t)
-        load_wg(wg1_t, wg1, 2 * S + HALF, 3 * S)
-        load_wg(wg1_t, wg1, 3 * S, 3 * S + HALF)
+        load_wg1(wg1_t, 0, 3, *UNITS[2])
         list4 = load_list(offs4, "list4")
         gain_t = load_channel_vector(gain, "gain_t")
         scl_t = []
@@ -171,13 +169,12 @@ def tile_list_phonon_mode_weave_kernel(
                     )
             return acc[:, 0 : j1 - j0]
 
-        def stream1_values(i, j0, j1, b, weighted=None):
+        def stream1_values(i, j0, j1, b):
             sums = sum_squares(i, j0, j1, b)
-            h1 = keep.tile([P, j1 - j0], F32, name="h1_%d_%d" % (i, j0))
+            h1 = keep.tile([P, j1 - j0], F32, name="h1_%d_%d" % (i, j0), align_bytes=64)
             nc.scalar.activation(h1[:], sums, ACT.Sqrt, bias=floor_t[:, i : i + 1])
-            weighted = h1 if weighted is None else weighted
-            nc.gpsimd.tensor_tensor(weighted[:], h1[:], wg1_t[:, S * i + j0 : S * i + j1], MULT)
-            return weighted
+            nc.gpsimd.tensor_tensor(h1[:], h1[:], wg1_t[:, S * i + j0 : S * i + j1], MULT)
+            return h1
 
         def stream1_put(i, j0, j1, h1):
             nc.vector.tensor_copy(pages[i][:].indirect(list3[:, j0 // 16 : j1 // 16]), h1[:])
@@ -185,40 +182,39 @@ def tile_list_phonon_mode_weave_kernel(
         def stream1(i, j0, j1, b):
             stream1_put(i, j0, j1, stream1_values(i, j0, j1, b))
 
+        last = PACK - 1
         project(0, (0, 1, 2, 3))
-        stream1(0, *UNITS[0], 0)
-        stream1(1, *UNITS[0], 1)
+        for i in range(PACK):
+            stream1(i, *UNITS[0], i)
         project(1, (4, 5, 6, 7))
-        stream1(0, *UNITS[1], 4)
-        stream1(1, *UNITS[1], 5)
-        project(2, (2, 3, 6, 7, 0, 1, 4, 5))
-        stream1(0, *UNITS[2], 2)
-        stream1(1, *UNITS[2], 3)
-        stream1(2, 0, HALF, 6)
+        for i in range(PACK):
+            stream1(i, *UNITS[1], 4 + i)
+        project(2, range(8))
+        stream1(0, *UNITS[2], 0)
         grouped = keep.tile([P, 2, PACK * H], BF16, name="w3_bf16", tag="w3_bf16", align_bytes=64)
         for a in range(2):
             nc.scalar.copy(
                 grouped[:, a, :].rearrange("p (i m j) -> p m i j", i=PACK, j=PACK),
                 w3_raw[a][:].rearrange("p j (m i) -> p m i j", i=PACK),
             )
-        w3_w = keep.tile([P, 2 * H], U32, name="w3_w", align_bytes=64)
+        w3_w = keep.tile([P, 2 * H], U32, name="w3_w", tag="h1_0_%d" % HALF, align_bytes=64)
         w3_plane = keep.tile([P, 2 * H], U8, name="w3_plane", align_bytes=64)
         nc.vector.quantize_mx(out=w3_w[:].bitcast(FP8X4), scales=w3_plane[:], in_=grouped[:].rearrange("p a c -> p (a c)"))
 
-        last = PACK - 1
-        stream1(2, HALF, S, 7)
-        after_w3 = keep.tile([P, HALF], F32, name="after_w3", tag="w3_bf16", align_bytes=64)
-        stream1_put(last, 0, HALF, stream1_values(last, 0, HALF, 0, after_w3))
-        h1_last = stream1_values(last, HALF, S, 1)
+        stream1(1, *UNITS[2], 1)
+        stream1(2, *UNITS[2], 2)
+        h1_last = stream1_values(last, HALF, S, 3)
+        after_w3 = keep.tile([P, S], F32, name="after_w3", tag="w3_bf16", align_bytes=64)
 
         starts = [sum(WIDTHS[:c]) for c in range(len(WIDTHS))]
         chunk_cols = [slice(starts[c], starts[c] + WIDTHS[c]) for c in range(len(WIDTHS))]
         z = [keep.tile([P, width, PACK], BF16, name="z", tag="z%d" % c, align_bytes=64) for c, width in enumerate(WIDTHS)]
 
         for i in range(PACK):
-            nc.gpsimd.tensor_tensor(scl_t[i][:], scl_t[i][:], wg2_t[:, S * i : S * (i + 1)], MULT)
+            weighted = after_w3 if i == 0 else scl_t[i]
+            nc.gpsimd.tensor_tensor(weighted[:], scl_t[i][:], wg2_t[:, S * i : S * (i + 1)], MULT)
             for h in range(2):
-                acc = bank((2 + 2 * i + h) % 8)
+                acc = bank((4 + 2 * i + h) % 8)
                 cols = slice(HALF * h, HALF * (h + 1))
                 for a in range(2):
                     nc.tensor.matmul_mx(
@@ -232,8 +228,8 @@ def tile_list_phonon_mode_weave_kernel(
                     )
                 h2 = keep.tile([P, BANK], F32, name="h2", tag="bank_copy", bufs=16)
                 nc.scalar.copy(h2[:], acc[:])
-                nc.gpsimd.tensor_tensor(scl_t[i][:, cols], scl_t[i][:, cols], h2[:], MULT)
-            nc.vector.tensor_copy(pages[i][:].indirect(list4[:]), scl_t[i][:])
+                nc.gpsimd.tensor_tensor(weighted[:, cols], weighted[:, cols], h2[:], MULT)
+            nc.vector.tensor_copy(pages[i][:].indirect(list4[:]), weighted[:])
             if i < last:
                 gain_col = keep.tile([P, 1], F32, name="gain_col")
                 nc.scalar.copy(gain_col[:], gain_t[:, i : i + 1])
@@ -271,13 +267,12 @@ def tile_list_phonon_mode_weave_kernel(
             return t
 
         final = len(WIDTHS) - 1
-        nc.scalar.activation(z[final][:, :, last], pages[last][:, chunk_cols[final]], ACT.Copy, scale=gain_col[:])
+        nc.scalar.activation(z[2][:, :, last], pages[last][:, chunk_cols[2]], ACT.Copy, scale=gain_col[:])
         filled = 0
         for c in range(final - 1):
             width = WIDTHS[c]
-            if c == 2:
-                gain_col = gain_after(0)
-            nc.vector.tensor_scalar_mul(z[c][:, :, last], pages[last][:, chunk_cols[c]], gain_col[:])
+            if c < 2:
+                nc.vector.tensor_scalar_mul(z[c][:, :, last], pages[last][:, chunk_cols[c]], gain_col[:])
             quantise(c)
             groups = BANK // width
             for m0 in range(0, N // P, groups):
@@ -289,9 +284,11 @@ def tile_list_phonon_mode_weave_kernel(
                 nc.sync.dma_start(out_rows[:, m0 : m0 + groups, chunk_cols[c]], res[:])
                 filled = filled + 1
 
-        nc.vector.tensor_scalar_mul(z[final - 1][:, :, last], pages[last][:, chunk_cols[final - 1]], gain_col[:])
-        quantise(final)
+        gain_col = gain_after(0)
+        for c in (final - 1, final):
+            nc.vector.tensor_scalar_mul(z[c][:, :, last], pages[last][:, chunk_cols[c]], gain_col[:])
         quantise(final - 1)
+        quantise(final)
         for m in range(N // P):
             res = keep.tile([P, 2 * BANK], F32, name="res_pair", tag="row4k_%d" % m)
             left = bank(2 * m)

@@ -16,6 +16,7 @@ FP8X4 = mybir.dt.float8_e4m3fn_x4
 FP4X4 = mybir.dt.float4_e2m1fn_x4
 ACT = mybir.ActivationFunctionType
 MULT = mybir.AluOpType.mult
+ADD = mybir.AluOpType.add
 
 P = 128
 PACK = 4
@@ -67,10 +68,10 @@ def tile_list_phonon_mode_weave_kernel(
             for q in (0, 2, 1, 3):
                 nc.sync.dma_start(t[32 * q : 32 * q + 32, c0:c1], rows)
 
-        def load_wg1(t, i0, i1, j0, j1):
-            rows = wg1.rearrange("(q i) j -> q i j", i=PACK)[:, i0:i1, j0:j1]
-            for q in (0, 2, 1, 3):
-                nc.sync.dma_start(t[:].rearrange("p (i j) -> p i j", i=PACK)[32 * q : 32 * q + 32, i0:i1, j0:j1], rows)
+        def load_w3(a):
+            t = keep.tile([P, PACK, H], F32, name="w3_raw%d" % a)
+            nc.sync.dma_start(t[:], w3[512 * a : 512 * (a + 1), :].rearrange("(p j) c -> p j c", j=PACK))
+            return t
 
         def load_channel_vector(src, name):
             t = keep.tile([P, PACK], F32, name=name)
@@ -100,15 +101,13 @@ def tile_list_phonon_mode_weave_kernel(
         wg1_t = keep.tile([P, PACK * S], F32, name="wg1_t")
         wg2_t = keep.tile([P, PACK * S], F32, name="wg2_t")
         tab2_w.append(load_words(tab2_words[1], T, "tab2_w1"))
-        load_wg1(wg1_t, 0, 2, *UNITS[0])
-        load_wg1(wg1_t, 2, 4, *UNITS[0])
-        load_wg1(wg1_t, 0, 4, *UNITS[1])
-        w3_raw = []
-        for a in range(2):
-            t = keep.tile([P, PACK, H], F32, name="w3_raw%d" % a)
-            nc.sync.dma_start(t[:], w3[512 * a : 512 * (a + 1), :].rearrange("(p j) c -> p j c", j=PACK))
-            w3_raw.append(t)
-        load_wg1(wg1_t, 0, 3, *UNITS[2])
+        for i in range(3):
+            load_wg(wg1_t, wg1, S * i, S * i + HALF)
+        w3_raw = [load_w3(0)]
+        load_wg(wg1_t, wg1, 3 * S, 3 * S + HALF)
+        w3_raw.append(load_w3(1))
+        for i in range(PACK):
+            load_wg(wg1_t, wg1, S * i + HALF, S * (i + 1))
         list4 = load_list(offs4, "list4")
         gain_t = load_channel_vector(gain, "gain_t")
         scl_t = []
@@ -117,7 +116,6 @@ def tile_list_phonon_mode_weave_kernel(
             nc.sync.dma_start(t[:], scl.rearrange("(p i) j -> p i j", i=PACK)[:, i, :])
             scl_t.append(t)
             load_wg(wg2_t, wg2, S * i, S * (i + 1))
-        load_wg(wg1_t, wg1, 3 * S + HALF, PACK * S)
         w4_w = load_words(w4_words[0], N, "w4_w")
         load_scales(nc.sync, w4_plane, w4_scales)
 
@@ -169,12 +167,13 @@ def tile_list_phonon_mode_weave_kernel(
                     )
             return acc[:, 0 : j1 - j0]
 
-        def stream1_values(i, j0, j1, b):
+        def stream1_values(i, j0, j1, b, weighted=None):
             sums = sum_squares(i, j0, j1, b)
             h1 = keep.tile([P, j1 - j0], F32, name="h1_%d_%d" % (i, j0), align_bytes=64)
             nc.scalar.activation(h1[:], sums, ACT.Sqrt, bias=floor_t[:, i : i + 1])
-            nc.gpsimd.tensor_tensor(h1[:], h1[:], wg1_t[:, S * i + j0 : S * i + j1], MULT)
-            return h1
+            weighted = h1 if weighted is None else weighted
+            nc.gpsimd.tensor_tensor(weighted[:], h1[:], wg1_t[:, S * i + j0 : S * i + j1], MULT)
+            return weighted
 
         def stream1_put(i, j0, j1, h1):
             nc.vector.tensor_copy(pages[i][:].indirect(list3[:, j0 // 16 : j1 // 16]), h1[:])
@@ -184,13 +183,13 @@ def tile_list_phonon_mode_weave_kernel(
 
         last = PACK - 1
         project(0, (0, 1, 2, 3))
-        for i in range(PACK):
-            stream1(i, *UNITS[0], i)
+        stream1(0, *UNITS[0], 0)
         project(1, (4, 5, 6, 7))
-        for i in range(PACK):
-            stream1(i, *UNITS[1], 4 + i)
-        project(2, range(8))
-        stream1(0, *UNITS[2], 0)
+        stream1(0, *UNITS[1], 1)
+        for i in range(1, PACK):
+            stream1(i, 0, HALF, 1 + i)
+        project(2, (5, 6, 7, 0, 1, 2, 3, 4))
+        stream1(0, HALF, S, 5)
         grouped = keep.tile([P, 2, PACK * H], BF16, name="w3_bf16", tag="w3_bf16", align_bytes=64)
         for a in range(2):
             nc.scalar.copy(
@@ -201,20 +200,20 @@ def tile_list_phonon_mode_weave_kernel(
         w3_plane = keep.tile([P, 2 * H], U8, name="w3_plane", align_bytes=64)
         nc.vector.quantize_mx(out=w3_w[:].bitcast(FP8X4), scales=w3_plane[:], in_=grouped[:].rearrange("p a c -> p (a c)"))
 
-        stream1(1, *UNITS[2], 1)
-        stream1(2, *UNITS[2], 2)
-        h1_last = stream1_values(last, HALF, S, 3)
-        after_w3 = keep.tile([P, S], F32, name="after_w3", tag="w3_bf16", align_bytes=64)
+        stream1(1, HALF, S, 6)
+        after_w3 = keep.tile([P, HALF], F32, name="after_w3", tag="w3_bf16", align_bytes=64)
+        stream1_put(2, HALF, S, stream1_values(2, HALF, S, 7, after_w3))
+        stream1(last, HALF, S, 0)
 
         starts = [sum(WIDTHS[:c]) for c in range(len(WIDTHS))]
         chunk_cols = [slice(starts[c], starts[c] + WIDTHS[c]) for c in range(len(WIDTHS))]
         z = [keep.tile([P, width, PACK], BF16, name="z", tag="z%d" % c, align_bytes=64) for c, width in enumerate(WIDTHS)]
 
         for i in range(PACK):
-            weighted = after_w3 if i == 0 else scl_t[i]
+            weighted = scl_t[i]
             nc.gpsimd.tensor_tensor(weighted[:], scl_t[i][:], wg2_t[:, S * i : S * (i + 1)], MULT)
             for h in range(2):
-                acc = bank((4 + 2 * i + h) % 8)
+                acc = bank((2 + 2 * i + h) % 8)
                 cols = slice(HALF * h, HALF * (h + 1))
                 for a in range(2):
                     nc.tensor.matmul_mx(
@@ -226,7 +225,10 @@ def tile_list_phonon_mode_weave_kernel(
                         start=(a == 0),
                         stop=(a == 1),
                     )
-                h2 = keep.tile([P, BANK], F32, name="h2", tag="bank_copy", bufs=16)
+                if i == last and h == 1:
+                    h2 = keep.tile([P, BANK], F32, name="h2_last")
+                else:
+                    h2 = keep.tile([P, BANK], F32, name="h2", tag="bank_copy", bufs=16)
                 nc.scalar.copy(h2[:], acc[:])
                 nc.gpsimd.tensor_tensor(weighted[:, cols], weighted[:, cols], h2[:], MULT)
             nc.vector.tensor_copy(pages[i][:].indirect(list4[:]), weighted[:])
@@ -234,9 +236,15 @@ def tile_list_phonon_mode_weave_kernel(
                 gain_col = keep.tile([P, 1], F32, name="gain_col")
                 nc.scalar.copy(gain_col[:], gain_t[:, i : i + 1])
                 for c, cols in enumerate(chunk_cols):
-                    nc.scalar.activation(z[c][:, :, i], pages[i][:, cols], ACT.Copy, scale=gain_col[:])
+                    if i < last - 1 or c < 3:
+                        nc.scalar.activation(z[c][:, :, i], pages[i][:, cols], ACT.Copy, scale=gain_col[:])
+        gain_pool = keep.tile([P, 1], F32, name="gain_pool", tag="h2_last")
+        nc.gpsimd.tensor_copy(gain_pool[:], gain_t[:, last - 1 : last])
+        for c in (3, 4):
+            nc.gpsimd.tensor_scalar(z[c][:, :, last - 1], pages[last - 1][:, chunk_cols[c]], gain_pool[:], 0.0, MULT, ADD)
+        gain_pool = keep.tile([P, 1], F32, name="gain_pool", tag="h2_last")
+        nc.gpsimd.tensor_copy(gain_pool[:], gain_t[:, last : last + 1])
 
-        stream1_put(last, HALF, S, h1_last)
         gain_col = keep.tile([P, 1], F32, name="gain_col")
         nc.scalar.copy(gain_col[:], gain_t[:, last : last + 1])
         z_w = keep.tile([P, T], U32, name="z_w", align_bytes=64)
@@ -263,7 +271,7 @@ def tile_list_phonon_mode_weave_kernel(
 
         def gain_after(c):
             t = keep.tile([P, 1], F32, name="gain_late", tag="z%d" % c, align_bytes=64)
-            nc.gpsimd.tensor_copy(t[:], gain_t[:, last : last + 1])
+            nc.gpsimd.tensor_copy(t[:], gain_pool[:])
             return t
 
         final = len(WIDTHS) - 1

@@ -82,8 +82,8 @@ def tile_list_phonon_mode_weave_kernel(
         nc.vector.memset(tab_plane[:, 0:S].bitcast(I32), 0)
         nc.gpsimd.memset(tab_plane[:, S:T].bitcast(I32), 0)
         wri_plane = scale_plane(nc.vector, 2 * H, "wri_plane")
-        tab2_plane = scale_plane(nc.gpsimd, T, "tab2_plane")
-        w4_plane = scale_plane(nc.gpsimd, N, "w4_plane")
+        tab2_plane = scale_plane(nc.vector, T, "tab2_plane")
+        w4_plane = scale_plane(nc.vector, N, "w4_plane")
         ident = keep.tile([P, P], F32, name="ident")
         make_identity(nc, ident[:])
 
@@ -100,8 +100,9 @@ def tile_list_phonon_mode_weave_kernel(
         list3 = load_list(offs3, "list3")
         wg1_t = keep.tile([P, PACK * S], F32, name="wg1_t")
         wg2_t = keep.tile([P, PACK * S], F32, name="wg2_t")
+        load_wg(wg1_t, wg1, 0, HALF)
         tab2_w.append(load_words(tab2_words[1], T, "tab2_w1"))
-        for i in range(3):
+        for i in range(1, 3):
             load_wg(wg1_t, wg1, S * i, S * i + HALF)
         w3_raw = [load_w3(0)]
         load_wg(wg1_t, wg1, 3 * S, 3 * S + HALF)
@@ -167,10 +168,20 @@ def tile_list_phonon_mode_weave_kernel(
                     )
             return acc[:, 0 : j1 - j0]
 
-        def stream1_values(i, j0, j1, b, weighted=None):
+        def magnitudes(i, j0, j1, b):
             sums = sum_squares(i, j0, j1, b)
             h1 = keep.tile([P, j1 - j0], F32, name="h1_%d_%d" % (i, j0), align_bytes=64)
             nc.scalar.activation(h1[:], sums, ACT.Sqrt, bias=floor_t[:, i : i + 1])
+            return h1
+
+        def stream1_fused(i, j0, j1, b):
+            h1 = magnitudes(i, j0, j1, b)
+            nc.vector.tensor_tensor(
+                pages[i][:].indirect(list3[:, j0 // 16 : j1 // 16]), h1[:], wg1_t[:, S * i + j0 : S * i + j1], MULT
+            )
+
+        def stream1_values(i, j0, j1, b, weighted=None):
+            h1 = magnitudes(i, j0, j1, b)
             weighted = h1 if weighted is None else weighted
             nc.gpsimd.tensor_tensor(weighted[:], h1[:], wg1_t[:, S * i + j0 : S * i + j1], MULT)
             return weighted
@@ -183,13 +194,15 @@ def tile_list_phonon_mode_weave_kernel(
 
         last = PACK - 1
         project(0, (0, 1, 2, 3))
-        stream1(0, *UNITS[0], 0)
-        project(1, (4, 5, 6, 7))
-        stream1(0, *UNITS[1], 1)
-        for i in range(1, PACK):
-            stream1(i, 0, HALF, 1 + i)
-        project(2, (5, 6, 7, 0, 1, 2, 3, 4))
-        stream1(0, HALF, S, 5)
+        stream1_fused(0, *UNITS[0], 4)
+        project(1, (0, 1, 2, 3))
+        stream1_fused(0, *UNITS[1], 5)
+        after_fused = keep.tile([P, HALF], F32, name="after_fused", tag="h1_0_%d" % UNITS[1][0], align_bytes=64)
+        stream1_put(1, 0, HALF, stream1_values(1, 0, HALF, 6, after_fused))
+        stream1(2, 0, HALF, 7)
+        stream1(3, 0, HALF, 4)
+        project(2, (0, 1, 2, 3, 5, 6, 7, 4))
+        stream1(0, HALF, S, 0)
         grouped = keep.tile([P, 2, PACK * H], BF16, name="w3_bf16", tag="w3_bf16", align_bytes=64)
         for a in range(2):
             nc.scalar.copy(
@@ -200,10 +213,10 @@ def tile_list_phonon_mode_weave_kernel(
         w3_plane = keep.tile([P, 2 * H], U8, name="w3_plane", align_bytes=64)
         nc.vector.quantize_mx(out=w3_w[:].bitcast(FP8X4), scales=w3_plane[:], in_=grouped[:].rearrange("p a c -> p (a c)"))
 
-        stream1(1, HALF, S, 6)
+        stream1(1, HALF, S, 1)
         after_w3 = keep.tile([P, HALF], F32, name="after_w3", tag="w3_bf16", align_bytes=64)
-        stream1_put(2, HALF, S, stream1_values(2, HALF, S, 7, after_w3))
-        stream1(last, HALF, S, 0)
+        stream1_put(2, HALF, S, stream1_values(2, HALF, S, 2, after_w3))
+        stream1(last, HALF, S, 3)
 
         starts = [sum(WIDTHS[:c]) for c in range(len(WIDTHS))]
         chunk_cols = [slice(starts[c], starts[c] + WIDTHS[c]) for c in range(len(WIDTHS))]
@@ -213,7 +226,7 @@ def tile_list_phonon_mode_weave_kernel(
             weighted = scl_t[i]
             nc.gpsimd.tensor_tensor(weighted[:], scl_t[i][:], wg2_t[:, S * i : S * (i + 1)], MULT)
             for h in range(2):
-                acc = bank((2 + 2 * i + h) % 8)
+                acc = bank((4 + 2 * i + h) % 8)
                 cols = slice(HALF * h, HALF * (h + 1))
                 for a in range(2):
                     nc.tensor.matmul_mx(

@@ -20,11 +20,19 @@ ADD = mybir.AluOpType.add
 
 P = 128
 PACK = 4
+LAST = PACK - 1
+K_PASS = P * PACK
+QUAD = 32
+QUADS = (0, 2, 1, 3)
 BANK = 512
+BANKS = 8
+LANES = 16
 HALF = S // 2
-LIST_COLS = S // 16
+FIRST = S // 4
+BANK_COPIES = 16
 WIDTHS = (256, 256, 512, 512, 512)
-UNITS = ((0, 256), (256, 512), (512, 1024))
+SCALAR_CHUNK = 2
+PAIR = (3, 4)
 
 
 def tile_list_phonon_mode_weave_kernel(
@@ -40,37 +48,42 @@ def tile_list_phonon_mode_weave_kernel(
         def bank(b):
             return psum.tile([P, BANK], F32, name="bank%d" % b)
 
+        def entries(list_tile, j0, j1):
+            return list_tile[:, j0 // LANES : j1 // LANES]
+
         def load_list(src, name):
-            t = lists.tile([P, LIST_COLS], U16, name=name)
+            t = lists.tile([P, S // LANES], U16, name=name)
             nc.sync.dma_start(t[:], src)
             return t
 
-        def scale_plane(engine, width, name):
+        def zeroed_plane(width, name):
             t = keep.tile([P, width], U8, name=name, align_bytes=64)
-            engine.memset(t[:].bitcast(I32), 0)
+            nc.vector.memset(t[:].bitcast(I32), 0)
             return t
 
-        def load_scales(queue, plane, src):
+        def load_scales(plane, src):
             for r in range(4):
-                queue.dma_start(plane[:].bitcast(I32)[r:P:32, :], src[0, r:16:4, :].bitcast(I32))
+                nc.sync.dma_start(plane[:].bitcast(I32)[r:P:QUAD, :], src[0, r:16:4, :].bitcast(I32))
 
         def load_scales_two_passes(plane, src):
-            for q in (0, 2, 1, 3):
-                nc.sync.dma_start(plane[:].bitcast(I32)[32 * q : 32 * q + 8, :], src[:, 4 * q : 4 * q + 4, :].bitcast(I32))
+            for q in QUADS:
+                nc.sync.dma_start(
+                    plane[:].bitcast(I32)[QUAD * q : QUAD * q + 8, :], src[:, 4 * q : 4 * q + 4, :].bitcast(I32)
+                )
 
         def load_words(src, width, name):
             t = keep.tile([P, width], I32, name=name, align_bytes=64)
             nc.sync.dma_start(t[:], src.rearrange("p t i -> p (t i)").bitcast(I32))
             return t
 
-        def load_wg(t, src, c0, c1):
-            rows = src.rearrange("(q i) j -> q (i j)", i=PACK)[:, c0:c1]
-            for q in (0, 2, 1, 3):
-                nc.sync.dma_start(t[32 * q : 32 * q + 32, c0:c1], rows)
+        def load_wg(t, src, i, j0, j1):
+            rows = src.rearrange("(q i) j -> q (i j)", i=PACK)[:, S * i + j0 : S * i + j1]
+            for q in QUADS:
+                nc.sync.dma_start(t[QUAD * q : QUAD * (q + 1), S * i + j0 : S * i + j1], rows)
 
         def load_w3(a):
             t = keep.tile([P, PACK, H], F32, name="w3_raw%d" % a)
-            nc.sync.dma_start(t[:], w3[512 * a : 512 * (a + 1), :].rearrange("(p j) c -> p j c", j=PACK))
+            nc.sync.dma_start(t[:], w3[K_PASS * a : K_PASS * (a + 1), :].rearrange("(p j) c -> p j c", j=PACK))
             return t
 
         def load_channel_vector(src, name):
@@ -79,19 +92,19 @@ def tile_list_phonon_mode_weave_kernel(
             return t
 
         tab_plane = keep.tile([P, T], U8, name="tab_plane", align_bytes=64)
-        nc.vector.memset(tab_plane[:, 0:S].bitcast(I32), 0)
-        nc.gpsimd.memset(tab_plane[:, S:T].bitcast(I32), 0)
-        wri_plane = scale_plane(nc.vector, 2 * H, "wri_plane")
-        tab2_plane = scale_plane(nc.vector, T, "tab2_plane")
-        w4_plane = scale_plane(nc.vector, N, "w4_plane")
+        nc.vector.memset(tab_plane[:, 0 : T // 2].bitcast(I32), 0)
+        nc.gpsimd.memset(tab_plane[:, T // 2 : T].bitcast(I32), 0)
+        wri_plane = zeroed_plane(2 * H, "wri_plane")
+        tab2_plane = zeroed_plane(T, "tab2_plane")
+        w4_plane = zeroed_plane(N, "w4_plane")
         ident = keep.tile([P, P], F32, name="ident")
         make_identity(nc, ident[:])
 
         list1 = load_list(offs, "list1")
         list2 = load_list(offs2, "list2")
-        load_scales(nc.sync, tab_plane, tab_scales)
+        load_scales(tab_plane, tab_scales)
         tab_w = load_words(tab_words[0], T, "tab_w")
-        load_scales(nc.sync, wri_plane, wri_scales)
+        load_scales(wri_plane, wri_scales)
         wri_w = keep.tile([P, 4 * H], U8, name="wri_w", align_bytes=64)
         nc.sync.dma_start(wri_w[:].bitcast(I32), wri_words[0].bitcast(I32))
         load_scales_two_passes(tab2_plane, tab2_scales)
@@ -100,25 +113,29 @@ def tile_list_phonon_mode_weave_kernel(
         list3 = load_list(offs3, "list3")
         wg1_t = keep.tile([P, PACK * S], F32, name="wg1_t")
         wg2_t = keep.tile([P, PACK * S], F32, name="wg2_t")
-        load_wg(wg1_t, wg1, 0, HALF)
+        first_rows = wg1.rearrange("(q i) j -> q i j", i=PACK)[:, 0:2, 0:FIRST]
+        for q in QUADS:
+            by_page = wg1_t[:].rearrange("p (i j) -> p i j", i=PACK)
+            nc.sync.dma_start(by_page[QUAD * q : QUAD * (q + 1), 0:2, 0:FIRST], first_rows)
         tab2_w.append(load_words(tab2_words[1], T, "tab2_w1"))
-        for i in range(1, 3):
-            load_wg(wg1_t, wg1, S * i, S * i + HALF)
-        w3_raw = [load_w3(0)]
-        load_wg(wg1_t, wg1, 3 * S, 3 * S + HALF)
-        w3_raw.append(load_w3(1))
-        for i in range(PACK):
-            load_wg(wg1_t, wg1, S * i + HALF, S * (i + 1))
+        for i in (2, 3):
+            load_wg(wg1_t, wg1, i, 0, HALF)
+        w3_raw = []
+        for i in (0, 1):
+            w3_raw.append(load_w3(i))
+            load_wg(wg1_t, wg1, i, FIRST, S)
+        for i in (2, 3):
+            load_wg(wg1_t, wg1, i, HALF, S)
         list4 = load_list(offs4, "list4")
         gain_t = load_channel_vector(gain, "gain_t")
         scl_t = []
         for i in range(PACK):
-            t = keep.tile([P, S], F32, name="scl", tag="row4k_%d" % i)
+            t = keep.tile([P, S], F32, name="scl", tag="wide_row%d" % i)
             nc.sync.dma_start(t[:], scl.rearrange("(p i) j -> p i j", i=PACK)[:, i, :])
             scl_t.append(t)
-            load_wg(wg2_t, wg2, S * i, S * (i + 1))
+            load_wg(wg2_t, wg2, i, 0, S)
         w4_w = load_words(w4_words[0], N, "w4_w")
-        load_scales(nc.sync, w4_plane, w4_scales)
+        load_scales(w4_plane, w4_scales)
 
         warm = keep.tile([P, 1], F32, name="warm")
         nc.scalar.activation(warm[:], ident[:, 0:1], ACT.Sqrt)
@@ -126,107 +143,120 @@ def tile_list_phonon_mode_weave_kernel(
         v_scale = keep.tile([P, S], U8, name="v_scale", align_bytes=64)
         nc.vector.tensor_copy(v_scale[:], tab_plane[:].indirect(list1[:]))
         v_w = []
-        for j0, j1 in UNITS:
+        for j0, j1 in ((0, FIRST), (FIRST, S)):
             t = keep.tile([P, j1 - j0], U32, name="v_w%d" % j0, align_bytes=64)
-            nc.vector.tensor_copy(t[:], tab_w[:].bitcast(U32).indirect(list1[:, j0 // 16 : j1 // 16]))
-            v_w.append(t)
+            nc.vector.tensor_copy(t[:], tab_w[:].bitcast(U32).indirect(entries(list1, j0, j1)))
+            v_w.extend(t[:, c : c + P] for c in range(0, j1 - j0, P))
         v2_w = [keep.tile([P, S], U32, name="v2_w%d" % a, align_bytes=64) for a in range(2)]
         v2_scale = keep.tile([P, S], U8, name="v2_scale", align_bytes=64)
         nc.vector.tensor_copy(v2_scale[:], tab2_plane[:].indirect(list2[:]))
-        nc.vector.tensor_copy(v2_w[0][:], tab2_w[0][:].bitcast(U32).indirect(list2[:]))
-        nc.vector.tensor_copy(v2_w[1][:], tab2_w[1][:].bitcast(U32).indirect(list2[:]))
+        for a in range(2):
+            nc.vector.tensor_copy(v2_w[a][:], tab2_w[a][:].bitcast(U32).indirect(list2[:]))
 
         pages = [keep.tile([P, T], F32, name="page%d" % i) for i in range(PACK)]
 
         squares = {}
 
-        def project(u, banks):
-            j0, j1 = UNITS[u]
-            for jb in range((j1 - j0) // P):
+        def project(j0, j1):
+            for jb in range(j0 // P, j1 // P):
                 for part in range(2):
-                    acc = bank(banks[2 * jb + part])
+                    acc = bank(2 * (jb - j0 // P) + part)
                     nc.tensor.matmul_mx(
                         out=acc[:],
-                        lhsT=v_w[u][:, P * jb : P * (jb + 1)].bitcast(FP8X4),
-                        lhsT_scale=v_scale[:, j0 + P * jb : j0 + P * (jb + 1)],
+                        lhsT=v_w[jb].bitcast(FP8X4),
+                        lhsT_scale=v_scale[:, P * jb : P * (jb + 1)],
                         rhs=wri_w[:, 2 * H * part : 2 * H * (part + 1)].bitcast(FP4X4),
                         rhs_scale=wri_plane[:, H * part : H * (part + 1)],
                         start=True,
                         stop=True,
                     )
-                    sq = keep.tile([P, PACK, P], F32, name="sq", tag="bank_copy", bufs=16)
+                    sq = keep.tile([P, PACK, P], F32, name="sq", tag="bank_copy", bufs=BANK_COPIES)
                     nc.scalar.activation(sq[:], acc[:].rearrange("j (p i) -> j i p", i=PACK), ACT.Square)
-                    squares[(j0 // P + jb, part)] = sq
+                    squares[(jb, part)] = sq
 
-        def sum_squares(i, j0, j1, b):
-            acc = bank(b)
-            for jb in range((j1 - j0) // P):
-                for part in range(2):
-                    nc.tensor.matmul(
-                        acc[:, P * jb : P * (jb + 1)], squares[(j0 // P + jb, part)][:, i, :], ident[:],
-                        start=(part == 0), stop=(part == 1), is_transpose=True,
-                    )
-            return acc[:, 0 : j1 - j0]
-
-        def magnitudes(i, j0, j1, b):
-            sums = sum_squares(i, j0, j1, b)
+        def magnitudes(i, j0, j1, first_bank):
             h1 = keep.tile([P, j1 - j0], F32, name="h1_%d_%d" % (i, j0), align_bytes=64)
-            nc.scalar.activation(h1[:], sums, ACT.Sqrt, bias=floor_t[:, i : i + 1])
+            cuts = (j0, HALF, j1) if j0 < HALF < j1 else (j0, j1)
+            for n, (c0, c1) in enumerate(zip(cuts, cuts[1:])):
+                acc = bank(first_bank + n)
+                for jb in range(c0 // P, c1 // P):
+                    for part in range(2):
+                        nc.tensor.matmul(
+                            acc[:, P * jb - c0 : P * (jb + 1) - c0], squares[(jb, part)][:, i, :], ident[:],
+                            start=(part == 0), stop=(part == 1), is_transpose=True,
+                        )
+                nc.scalar.activation(
+                    h1[:, c0 - j0 : c1 - j0], acc[:, 0 : c1 - c0], ACT.Sqrt, bias=floor_t[:, i : i + 1]
+                )
             return h1
 
-        def stream1_fused(i, j0, j1, b):
-            h1 = magnitudes(i, j0, j1, b)
+        def stream1_fused(i, j0, j1, first_bank):
+            h1 = magnitudes(i, j0, j1, first_bank)
             nc.vector.tensor_tensor(
-                pages[i][:].indirect(list3[:, j0 // 16 : j1 // 16]), h1[:], wg1_t[:, S * i + j0 : S * i + j1], MULT
+                pages[i][:].indirect(entries(list3, j0, j1)), h1[:], wg1_t[:, S * i + j0 : S * i + j1], MULT
             )
 
-        def stream1_values(i, j0, j1, b, weighted=None):
-            h1 = magnitudes(i, j0, j1, b)
+        def stream1(i, j0, j1, first_bank, weighted=None):
+            h1 = magnitudes(i, j0, j1, first_bank)
             weighted = h1 if weighted is None else weighted
             nc.gpsimd.tensor_tensor(weighted[:], h1[:], wg1_t[:, S * i + j0 : S * i + j1], MULT)
-            return weighted
+            nc.vector.tensor_copy(pages[i][:].indirect(entries(list3, j0, j1)), weighted[:])
 
-        def stream1_put(i, j0, j1, h1):
-            nc.vector.tensor_copy(pages[i][:].indirect(list3[:, j0 // 16 : j1 // 16]), h1[:])
+        project(0, FIRST)
+        stream1_fused(0, 0, FIRST, 4)
+        stream1_fused(1, 0, FIRST, 5)
+        project(FIRST, HALF)
+        after_fused = keep.tile([P, HALF], F32, name="after_fused", tag="h1_1_0", align_bytes=64)
+        stream1(2, 0, HALF, 6, after_fused)
+        stream1(3, 0, HALF, 7)
+        project(HALF, S)
+        stream1(0, FIRST, S, 0)
 
-        def stream1(i, j0, j1, b):
-            stream1_put(i, j0, j1, stream1_values(i, j0, j1, b))
-
-        last = PACK - 1
-        project(0, (0, 1, 2, 3))
-        stream1_fused(0, *UNITS[0], 4)
-        project(1, (0, 1, 2, 3))
-        stream1_fused(0, *UNITS[1], 5)
-        after_fused = keep.tile([P, HALF], F32, name="after_fused", tag="h1_0_%d" % UNITS[1][0], align_bytes=64)
-        stream1_put(1, 0, HALF, stream1_values(1, 0, HALF, 6, after_fused))
-        stream1(2, 0, HALF, 7)
-        stream1(3, 0, HALF, 4)
-        project(2, (0, 1, 2, 3, 5, 6, 7, 4))
-        stream1(0, HALF, S, 0)
-        grouped = keep.tile([P, 2, PACK * H], BF16, name="w3_bf16", tag="w3_bf16", align_bytes=64)
+        grouped = keep.tile([P, 2, PACK * H], BF16, name="w3_bf16", align_bytes=64)
         for a in range(2):
             nc.scalar.copy(
                 grouped[:, a, :].rearrange("p (i m j) -> p m i j", i=PACK, j=PACK),
                 w3_raw[a][:].rearrange("p j (m i) -> p m i j", i=PACK),
             )
-        w3_w = keep.tile([P, 2 * H], U32, name="w3_w", tag="h1_0_%d" % HALF, align_bytes=64)
+        w3_w = keep.tile([P, 2 * H], U32, name="w3_w", tag="h1_0_%d" % FIRST, align_bytes=64)
         w3_plane = keep.tile([P, 2 * H], U8, name="w3_plane", align_bytes=64)
-        nc.vector.quantize_mx(out=w3_w[:].bitcast(FP8X4), scales=w3_plane[:], in_=grouped[:].rearrange("p a c -> p (a c)"))
+        nc.vector.quantize_mx(
+            out=w3_w[:].bitcast(FP8X4), scales=w3_plane[:], in_=grouped[:].rearrange("p a c -> p (a c)")
+        )
 
-        stream1(1, HALF, S, 1)
+        stream1(1, FIRST, S, 2)
         after_w3 = keep.tile([P, HALF], F32, name="after_w3", tag="w3_bf16", align_bytes=64)
-        stream1_put(2, HALF, S, stream1_values(2, HALF, S, 2, after_w3))
-        stream1(last, HALF, S, 3)
+        stream1(2, HALF, S, 4, after_w3)
+        stream1(3, HALF, S, 5)
 
         starts = [sum(WIDTHS[:c]) for c in range(len(WIDTHS))]
         chunk_cols = [slice(starts[c], starts[c] + WIDTHS[c]) for c in range(len(WIDTHS))]
-        z = [keep.tile([P, width, PACK], BF16, name="z", tag="z%d" % c, align_bytes=64) for c, width in enumerate(WIDTHS)]
+        z = [
+            keep.tile([P, width, PACK], BF16, name="z", tag="z%d" % c, align_bytes=64)
+            for c, width in enumerate(WIDTHS)
+        ]
 
+        def gain_on_scalar(i):
+            t = keep.tile([P, 1], F32, name="gain_col")
+            nc.scalar.copy(t[:], gain_t[:, i : i + 1])
+            return t
+
+        def gain_on_gpsimd(i):
+            t = keep.tile([P, 1], F32, name="gain_pool", tag="h2_last")
+            nc.gpsimd.tensor_copy(t[:], gain_t[:, i : i + 1])
+            return t
+
+        def slot_on_scalar(c, i, gain_col):
+            nc.scalar.activation(z[c][:, :, i], pages[i][:, chunk_cols[c]], ACT.Copy, scale=gain_col[:])
+
+        def last_slot_on_vector(c, gain_col):
+            nc.vector.tensor_scalar_mul(z[c][:, :, LAST], pages[LAST][:, chunk_cols[c]], gain_col[:])
+
+        first_h2_bank = 6
         for i in range(PACK):
-            weighted = scl_t[i]
-            nc.gpsimd.tensor_tensor(weighted[:], scl_t[i][:], wg2_t[:, S * i : S * (i + 1)], MULT)
+            nc.gpsimd.tensor_tensor(scl_t[i][:], scl_t[i][:], wg2_t[:, S * i : S * (i + 1)], MULT)
             for h in range(2):
-                acc = bank((4 + 2 * i + h) % 8)
+                acc = bank((first_h2_bank + 2 * i + h) % BANKS)
                 cols = slice(HALF * h, HALF * (h + 1))
                 for a in range(2):
                     nc.tensor.matmul_mx(
@@ -238,28 +268,27 @@ def tile_list_phonon_mode_weave_kernel(
                         start=(a == 0),
                         stop=(a == 1),
                     )
-                if i == last and h == 1:
+                if i == LAST and h == 1:
                     h2 = keep.tile([P, BANK], F32, name="h2_last")
                 else:
-                    h2 = keep.tile([P, BANK], F32, name="h2", tag="bank_copy", bufs=16)
+                    h2 = keep.tile([P, BANK], F32, name="h2", tag="bank_copy", bufs=BANK_COPIES)
                 nc.scalar.copy(h2[:], acc[:])
-                nc.gpsimd.tensor_tensor(weighted[:, cols], weighted[:, cols], h2[:], MULT)
-            nc.vector.tensor_copy(pages[i][:].indirect(list4[:]), weighted[:])
-            if i < last:
-                gain_col = keep.tile([P, 1], F32, name="gain_col")
-                nc.scalar.copy(gain_col[:], gain_t[:, i : i + 1])
-                for c, cols in enumerate(chunk_cols):
-                    if i < last - 1 or c < 3:
-                        nc.scalar.activation(z[c][:, :, i], pages[i][:, cols], ACT.Copy, scale=gain_col[:])
-        gain_pool = keep.tile([P, 1], F32, name="gain_pool", tag="h2_last")
-        nc.gpsimd.tensor_copy(gain_pool[:], gain_t[:, last - 1 : last])
-        for c in (3, 4):
-            nc.gpsimd.tensor_scalar(z[c][:, :, last - 1], pages[last - 1][:, chunk_cols[c]], gain_pool[:], 0.0, MULT, ADD)
-        gain_pool = keep.tile([P, 1], F32, name="gain_pool", tag="h2_last")
-        nc.gpsimd.tensor_copy(gain_pool[:], gain_t[:, last : last + 1])
+                nc.gpsimd.tensor_tensor(scl_t[i][:, cols], scl_t[i][:, cols], h2[:], MULT)
+            nc.vector.tensor_copy(pages[i][:].indirect(list4[:]), scl_t[i][:])
+            if i < LAST:
+                gain_col = gain_on_scalar(i)
+                for c in range(len(WIDTHS)):
+                    if i < LAST - 1 or c not in PAIR:
+                        slot_on_scalar(c, i, gain_col)
 
-        gain_col = keep.tile([P, 1], F32, name="gain_col")
-        nc.scalar.copy(gain_col[:], gain_t[:, last : last + 1])
+        gain_pool = gain_on_gpsimd(LAST - 1)
+        for c in PAIR:
+            nc.gpsimd.tensor_scalar(
+                z[c][:, :, LAST - 1], pages[LAST - 1][:, chunk_cols[c]], gain_pool[:], 0.0, MULT, ADD
+            )
+        gain_pool = gain_on_gpsimd(LAST)
+        gain_col = gain_on_scalar(LAST)
+
         z_w = keep.tile([P, T], U32, name="z_w", align_bytes=64)
         z_plane = keep.tile([P, T], U8, name="z_plane", align_bytes=64)
         out_rows = out.rearrange("(m p) t -> p m t", p=P)
@@ -282,43 +311,38 @@ def tile_list_phonon_mode_weave_kernel(
                 stop=True,
             )
 
-        def gain_after(c):
-            t = keep.tile([P, 1], F32, name="gain_late", tag="z%d" % c, align_bytes=64)
-            nc.gpsimd.tensor_copy(t[:], gain_pool[:])
-            return t
-
-        final = len(WIDTHS) - 1
-        nc.scalar.activation(z[2][:, :, last], pages[last][:, chunk_cols[2]], ACT.Copy, scale=gain_col[:])
-        filled = 0
-        for c in range(final - 1):
+        slot_on_scalar(SCALAR_CHUNK, LAST, gain_col)
+        next_bank = 0
+        for c in range(PAIR[0]):
             width = WIDTHS[c]
-            if c < 2:
-                nc.vector.tensor_scalar_mul(z[c][:, :, last], pages[last][:, chunk_cols[c]], gain_col[:])
+            if c != SCALAR_CHUNK:
+                last_slot_on_vector(c, gain_col)
             quantise(c)
             groups = BANK // width
             for m0 in range(0, N // P, groups):
-                acc = bank(filled)
+                acc = bank(next_bank)
                 for g in range(groups):
                     product(acc[:, width * g : width * (g + 1)], m0 + g, c)
-                res = keep.tile([P, groups, width], F32, name="res", tag="bank_copy", bufs=16)
+                res = keep.tile([P, groups, width], F32, name="res", tag="bank_copy", bufs=BANK_COPIES)
                 nc.scalar.copy(res[:].rearrange("p g t -> p (g t)"), acc[:])
                 nc.sync.dma_start(out_rows[:, m0 : m0 + groups, chunk_cols[c]], res[:])
-                filled = filled + 1
+                next_bank = next_bank + 1
 
-        gain_col = gain_after(0)
-        for c in (final - 1, final):
-            nc.vector.tensor_scalar_mul(z[c][:, :, last], pages[last][:, chunk_cols[c]], gain_col[:])
-        quantise(final - 1)
-        quantise(final)
+        gain_late = keep.tile([P, 1], F32, name="gain_late", tag="z0", align_bytes=64)
+        nc.gpsimd.tensor_copy(gain_late[:], gain_pool[:])
+        for c in PAIR:
+            last_slot_on_vector(c, gain_late)
+        for c in PAIR:
+            quantise(c)
         for m in range(N // P):
-            res = keep.tile([P, 2 * BANK], F32, name="res_pair", tag="row4k_%d" % m)
+            res = keep.tile([P, 2 * BANK], F32, name="res_pair", tag="wide_row%d" % m)
             left = bank(2 * m)
-            product(left[:], m, final - 1)
+            product(left[:], m, PAIR[0])
             nc.vector.tensor_copy(res[:, 0:BANK], left[:])
             right = bank(2 * m + 1)
-            product(right[:], m, final)
+            product(right[:], m, PAIR[1])
             if m == 0:
                 nc.vector.tensor_copy(res[:, BANK : 2 * BANK], right[:])
             else:
                 nc.scalar.copy(res[:, BANK : 2 * BANK], right[:])
-            nc.sync.dma_start(out_rows[:, m, starts[final - 1] : T], res[:])
+            nc.sync.dma_start(out_rows[:, m, starts[PAIR[0]] : T], res[:])

@@ -1,7 +1,6 @@
 from contextlib import ExitStack
 
 import concourse.mybir as mybir
-from concourse.masks import make_identity
 
 K, K2, H, N, T, S = 512, 1024, 512, 512, 2048, 1024
 FLOPS = 2 * K * 2 * H * S + 2 * K2 * H * S + 2 * H * N * T
@@ -17,6 +16,7 @@ FP4X4 = mybir.dt.float4_e2m1fn_x4
 ACT = mybir.ActivationFunctionType
 MULT = mybir.AluOpType.mult
 ADD = mybir.AluOpType.add
+EQUAL = mybir.AluOpType.is_equal
 
 P = 128
 PACK = 4
@@ -98,7 +98,18 @@ def tile_list_phonon_mode_weave_kernel(
         tab2_plane = zeroed_plane(T, "tab2_plane")
         w4_plane = zeroed_plane(N, "w4_plane")
         ident = keep.tile([P, P], F32, name="ident")
-        make_identity(nc, ident[:])
+        nc.gpsimd.memset(ident[:], 0.0)
+        ones = keep.tile([P, QUAD], F32, name="ones")
+        nc.vector.memset(ones[:], 1.0)
+        count = keep.tile([P, QUAD], F32, name="count", align_bytes=64)
+        nc.vector.tensor_tensor_scan(count[:], ones[:], ones[:], 0.0, MULT, ADD)
+        turned = keep.tile([P, QUAD], F32, name="turned", align_bytes=64)
+        nc.vector.transpose(turned[:], count[:])
+        diagonal = keep.tile([P, QUAD], F32, name="diagonal")
+        nc.vector.tensor_tensor(diagonal[:], count[:], turned[:], EQUAL)
+        for q in range(P // QUAD):
+            rows = slice(QUAD * q, QUAD * (q + 1))
+            nc.scalar.copy(ident[rows, rows], diagonal[rows, :])
 
         list1 = load_list(offs, "list1")
         list2 = load_list(offs2, "list2")
@@ -138,7 +149,7 @@ def tile_list_phonon_mode_weave_kernel(
         load_scales(w4_plane, w4_scales)
 
         warm = keep.tile([P, 1], F32, name="warm")
-        nc.scalar.activation(warm[:], ident[:, 0:1], ACT.Sqrt)
+        nc.scalar.activation(warm[:], ones[:, 0:1], ACT.Sqrt)
 
         v_scale = keep.tile([P, S], U8, name="v_scale", align_bytes=64)
         nc.vector.tensor_copy(v_scale[:], tab_plane[:].indirect(list1[:]))

@@ -31,7 +31,6 @@ HALF = S // 2
 FIRST = S // 4
 BANK_COPIES = 16
 WIDTHS = (256, 256, 512, 512, 512)
-SCALAR_CHUNK = 2
 PAIR = (3, 4)
 
 
@@ -257,11 +256,17 @@ def tile_list_phonon_mode_weave_kernel(
             nc.gpsimd.tensor_copy(t[:], gain_t[:, i : i + 1])
             return t
 
-        def slot_on_scalar(c, i, gain_col):
-            nc.scalar.activation(z[c][:, :, i], pages[i][:, chunk_cols[c]], ACT.Copy, scale=gain_col[:])
+        def slot_on_scalar(c, i, gain_col, t0=0, t1=None):
+            t1 = WIDTHS[c] if t1 is None else t1
+            nc.scalar.activation(
+                z[c][:, t0:t1, i], pages[i][:, starts[c] + t0 : starts[c] + t1], ACT.Copy, scale=gain_col[:]
+            )
 
-        def last_slot_on_vector(c, gain_col):
-            nc.vector.tensor_scalar_mul(z[c][:, :, LAST], pages[LAST][:, chunk_cols[c]], gain_col[:])
+        def last_slot_on_vector(c, gain_col, t0=0, t1=None):
+            t1 = WIDTHS[c] if t1 is None else t1
+            nc.vector.tensor_scalar_mul(
+                z[c][:, t0:t1, LAST], pages[LAST][:, starts[c] + t0 : starts[c] + t1], gain_col[:]
+            )
 
         first_h2_bank = 6
         for i in range(PACK):
@@ -322,35 +327,43 @@ def tile_list_phonon_mode_weave_kernel(
                 stop=True,
             )
 
-        slot_on_scalar(SCALAR_CHUNK, LAST, gain_col)
-        next_bank = 0
-        for c in range(PAIR[0]):
+        def emit(acc, m0, groups, c):
             width = WIDTHS[c]
-            if c != SCALAR_CHUNK:
-                last_slot_on_vector(c, gain_col)
-            quantise(c)
-            groups = BANK // width
-            for m0 in range(0, N // P, groups):
-                acc = bank(next_bank)
-                for g in range(groups):
-                    product(acc[:, width * g : width * (g + 1)], m0 + g, c)
-                res = keep.tile([P, groups, width], F32, name="res", tag="bank_copy", bufs=BANK_COPIES)
-                nc.scalar.copy(res[:].rearrange("p g t -> p (g t)"), acc[:])
-                nc.sync.dma_start(out_rows[:, m0 : m0 + groups, chunk_cols[c]], res[:])
-                next_bank = next_bank + 1
+            for g in range(groups):
+                product(acc[:, width * g : width * (g + 1)], m0 + g, c)
+            res = keep.tile([P, groups, width], F32, name="res", tag="bank_copy", bufs=BANK_COPIES)
+            nc.scalar.copy(res[:].rearrange("p g t -> p (g t)"), acc[:, 0 : groups * width])
+            nc.sync.dma_start(out_rows[:, m0 : m0 + groups, chunk_cols[c]], res[:])
+
+        last_slot_on_vector(0, gain_col, 0, P)
+        slot_on_scalar(0, LAST, gain_col, P, 2 * P)
+        slot_on_scalar(2, LAST, gain_col, 2 * P, 4 * P)
+        quantise(0)
+        emit(bank(0), 0, 1, 0)
+        emit(bank(1), 1, 1, 0)
+        emit(bank(2), 2, 2, 0)
+        last_slot_on_vector(1, gain_col, 0, P)
+        last_slot_on_vector(1, gain_col, P, 2 * P)
+        quantise(1)
+        emit(bank(3), 0, 2, 1)
+        emit(bank(4), 2, 2, 1)
+        last_slot_on_vector(2, gain_col, 0, 2 * P)
+        quantise(2)
+        for m in range(N // P):
+            emit(bank((5 + m) % BANKS), m, 1, 2)
 
         gain_late = keep.tile([P, 1], F32, name="gain_late", tag="z0", align_bytes=64)
-        nc.gpsimd.tensor_copy(gain_late[:], gain_pool[:])
+        nc.vector.tensor_copy(gain_late[:], gain_pool[:])
         for c in PAIR:
             last_slot_on_vector(c, gain_late)
         for c in PAIR:
             quantise(c)
         for m in range(N // P):
             res = keep.tile([P, 2 * BANK], F32, name="res_pair", tag="wide_row%d" % m)
-            left = bank(2 * m)
+            left = bank((2 * m + 1) % BANKS)
             product(left[:], m, PAIR[0])
             nc.vector.tensor_copy(res[:, 0:BANK], left[:])
-            right = bank(2 * m + 1)
+            right = bank((2 * m + 2) % BANKS)
             product(right[:], m, PAIR[1])
             if m == 0:
                 nc.vector.tensor_copy(res[:, BANK : 2 * BANK], right[:])

@@ -31,6 +31,7 @@ HALF = S // 2
 FIRST = S // 4
 BANK_COPIES = 16
 WIDTHS = (256, 256, 512, 512, 512)
+SCALAR_CHUNK = 2
 PAIR = (3, 4)
 
 
@@ -206,11 +207,17 @@ def tile_list_phonon_mode_weave_kernel(
                 pages[i][:].indirect(entries(list3, j0, j1)), h1[:], wg1_t[:, S * i + j0 : S * i + j1], MULT
             )
 
-        def stream1(i, j0, j1, first_bank, weighted=None):
+        def weigh(i, j0, j1, first_bank, weighted=None):
             h1 = magnitudes(i, j0, j1, first_bank)
             weighted = h1 if weighted is None else weighted
             nc.gpsimd.tensor_tensor(weighted[:], h1[:], wg1_t[:, S * i + j0 : S * i + j1], MULT)
+            return weighted
+
+        def scatter1(i, j0, j1, weighted):
             nc.vector.tensor_copy(pages[i][:].indirect(entries(list3, j0, j1)), weighted[:])
+
+        def stream1(i, j0, j1, first_bank, weighted=None):
+            scatter1(i, j0, j1, weigh(i, j0, j1, first_bank, weighted))
 
         project(0, FIRST)
         stream1_fused(0, 0, FIRST, 4)
@@ -221,6 +228,8 @@ def tile_list_phonon_mode_weave_kernel(
         stream1(3, 0, HALF, 7)
         project(HALF, S)
         stream1(0, FIRST, S, 0)
+        weighted1 = keep.tile([P, S - FIRST], F32, name="weighted1")
+        weigh(1, FIRST, S, 2, weighted1)
 
         grouped = keep.tile([P, 2, PACK * H], BF16, name="w3_bf16", align_bytes=64)
         for a in range(2):
@@ -228,13 +237,13 @@ def tile_list_phonon_mode_weave_kernel(
                 grouped[:, a, :].rearrange("p (i m j) -> p m i j", i=PACK, j=PACK),
                 w3_raw[a][:].rearrange("p j (m i) -> p m i j", i=PACK),
             )
-        w3_w = keep.tile([P, 2 * H], U32, name="w3_w", tag="h1_0_%d" % FIRST, align_bytes=64)
+        w3_w = keep.tile([P, 2 * H], U32, name="w3_w", tag="h1_1_%d" % FIRST, align_bytes=64)
         w3_plane = keep.tile([P, 2 * H], U8, name="w3_plane", align_bytes=64)
         nc.vector.quantize_mx(
             out=w3_w[:].bitcast(FP8X4), scales=w3_plane[:], in_=grouped[:].rearrange("p a c -> p (a c)")
         )
 
-        stream1(1, FIRST, S, 2)
+        scatter1(1, FIRST, S, weighted1)
         after_w3 = keep.tile([P, HALF], F32, name="after_w3", tag="w3_bf16", align_bytes=64)
         stream1(2, HALF, S, 4, after_w3)
         stream1(3, HALF, S, 5)
@@ -256,17 +265,11 @@ def tile_list_phonon_mode_weave_kernel(
             nc.gpsimd.tensor_copy(t[:], gain_t[:, i : i + 1])
             return t
 
-        def slot_on_scalar(c, i, gain_col, t0=0, t1=None):
-            t1 = WIDTHS[c] if t1 is None else t1
-            nc.scalar.activation(
-                z[c][:, t0:t1, i], pages[i][:, starts[c] + t0 : starts[c] + t1], ACT.Copy, scale=gain_col[:]
-            )
+        def slot_on_scalar(c, i, gain_col):
+            nc.scalar.activation(z[c][:, :, i], pages[i][:, chunk_cols[c]], ACT.Copy, scale=gain_col[:])
 
-        def last_slot_on_vector(c, gain_col, t0=0, t1=None):
-            t1 = WIDTHS[c] if t1 is None else t1
-            nc.vector.tensor_scalar_mul(
-                z[c][:, t0:t1, LAST], pages[LAST][:, starts[c] + t0 : starts[c] + t1], gain_col[:]
-            )
+        def last_slot_on_vector(c, gain_col):
+            nc.vector.tensor_scalar_mul(z[c][:, :, LAST], pages[LAST][:, chunk_cols[c]], gain_col[:])
 
         first_h2_bank = 6
         for i in range(PACK):
@@ -327,43 +330,35 @@ def tile_list_phonon_mode_weave_kernel(
                 stop=True,
             )
 
-        def emit(acc, m0, groups, c):
+        slot_on_scalar(SCALAR_CHUNK, LAST, gain_col)
+        next_bank = 0
+        for c in range(PAIR[0]):
             width = WIDTHS[c]
-            for g in range(groups):
-                product(acc[:, width * g : width * (g + 1)], m0 + g, c)
-            res = keep.tile([P, groups, width], F32, name="res", tag="bank_copy", bufs=BANK_COPIES)
-            nc.scalar.copy(res[:].rearrange("p g t -> p (g t)"), acc[:, 0 : groups * width])
-            nc.sync.dma_start(out_rows[:, m0 : m0 + groups, chunk_cols[c]], res[:])
-
-        last_slot_on_vector(0, gain_col, 0, P)
-        slot_on_scalar(0, LAST, gain_col, P, 2 * P)
-        slot_on_scalar(2, LAST, gain_col, 2 * P, 4 * P)
-        quantise(0)
-        emit(bank(0), 0, 1, 0)
-        emit(bank(1), 1, 1, 0)
-        emit(bank(2), 2, 2, 0)
-        last_slot_on_vector(1, gain_col, 0, P)
-        last_slot_on_vector(1, gain_col, P, 2 * P)
-        quantise(1)
-        emit(bank(3), 0, 2, 1)
-        emit(bank(4), 2, 2, 1)
-        last_slot_on_vector(2, gain_col, 0, 2 * P)
-        quantise(2)
-        for m in range(N // P):
-            emit(bank((5 + m) % BANKS), m, 1, 2)
+            if c != SCALAR_CHUNK:
+                last_slot_on_vector(c, gain_col)
+            quantise(c)
+            groups = BANK // width
+            for m0 in range(0, N // P, groups):
+                acc = bank(next_bank)
+                for g in range(groups):
+                    product(acc[:, width * g : width * (g + 1)], m0 + g, c)
+                res = keep.tile([P, groups, width], F32, name="res", tag="bank_copy", bufs=BANK_COPIES)
+                nc.scalar.copy(res[:].rearrange("p g t -> p (g t)"), acc[:])
+                nc.sync.dma_start(out_rows[:, m0 : m0 + groups, chunk_cols[c]], res[:])
+                next_bank = next_bank + 1
 
         gain_late = keep.tile([P, 1], F32, name="gain_late", tag="z0", align_bytes=64)
-        nc.vector.tensor_copy(gain_late[:], gain_pool[:])
+        nc.gpsimd.tensor_copy(gain_late[:], gain_pool[:])
         for c in PAIR:
             last_slot_on_vector(c, gain_late)
         for c in PAIR:
             quantise(c)
         for m in range(N // P):
             res = keep.tile([P, 2 * BANK], F32, name="res_pair", tag="wide_row%d" % m)
-            left = bank((2 * m + 1) % BANKS)
+            left = bank(2 * m)
             product(left[:], m, PAIR[0])
             nc.vector.tensor_copy(res[:, 0:BANK], left[:])
-            right = bank((2 * m + 2) % BANKS)
+            right = bank(2 * m + 1)
             product(right[:], m, PAIR[1])
             if m == 0:
                 nc.vector.tensor_copy(res[:, BANK : 2 * BANK], right[:])

@@ -337,13 +337,13 @@ def tile_list_phonon_mode_weave_kernel(
             if c != SCALAR_CHUNK:
                 last_slot_on_vector(c, gain_col)
             quantise(c)
-            groups = BANK // width
+            groups = 1 if c == 0 else BANK // width
             for m0 in range(0, N // P, groups):
-                acc = bank(next_bank)
+                acc = bank(next_bank % BANKS)
                 for g in range(groups):
                     product(acc[:, width * g : width * (g + 1)], m0 + g, c)
                 res = keep.tile([P, groups, width], F32, name="res", tag="bank_copy", bufs=BANK_COPIES)
-                nc.scalar.copy(res[:].rearrange("p g t -> p (g t)"), acc[:])
+                nc.scalar.copy(res[:].rearrange("p g t -> p (g t)"), acc[:, 0 : groups * width])
                 nc.sync.dma_start(out_rows[:, m0 : m0 + groups, chunk_cols[c]], res[:])
                 next_bank = next_bank + 1
 
@@ -355,13 +355,15 @@ def tile_list_phonon_mode_weave_kernel(
             quantise(c)
         for m in range(N // P):
             res = keep.tile([P, 2 * BANK], F32, name="res_pair", tag="wide_row%d" % m)
-            left = bank(2 * m)
+            left = bank((next_bank + 2 * m) % BANKS)
             product(left[:], m, PAIR[0])
             nc.vector.tensor_copy(res[:, 0:BANK], left[:])
-            right = bank(2 * m + 1)
+            right = bank((next_bank + 2 * m + 1) % BANKS)
             product(right[:], m, PAIR[1])
             if m == 0:
+                nc.sync.dma_start(out_rows[:, m, chunk_cols[PAIR[0]]], res[:, 0:BANK])
                 nc.vector.tensor_copy(res[:, BANK : 2 * BANK], right[:])
+                nc.sync.dma_start(out_rows[:, m, chunk_cols[PAIR[1]]], res[:, BANK : 2 * BANK])
             else:
                 nc.scalar.copy(res[:, BANK : 2 * BANK], right[:])
-            nc.sync.dma_start(out_rows[:, m, starts[PAIR[0]] : T], res[:])
+                nc.sync.dma_start(out_rows[:, m, starts[PAIR[0]] : T], res[:])

@@ -330,7 +330,18 @@ def tile_list_phonon_mode_weave_kernel(
                 stop=True,
             )
 
-        slot_on_scalar(SCALAR_CHUNK, LAST, gain_col)
+        gain_first = keep.tile([P, 1], F32, name="gain_first")
+        nc.scalar.copy(gain_first[:], gain_t[:, LAST : LAST + 1])
+        first = starts[SCALAR_CHUNK]
+        gain_late = None
+        for c0, c1 in ((0, P), (P, 2 * P), (2 * P, WIDTHS[SCALAR_CHUNK])):
+            if c0 == 2 * P:
+                gain_late = keep.tile([P, 1], F32, name="gain_late", tag="gain_first")
+                nc.scalar.copy(gain_late[:], gain_pool[:])
+            nc.scalar.activation(
+                z[SCALAR_CHUNK][:, c0:c1, LAST], pages[LAST][:, first + c0 : first + c1], ACT.Copy,
+                scale=gain_col[:] if c0 else gain_first[:],
+            )
         next_bank = 0
         for c in range(PAIR[0]):
             width = WIDTHS[c]
@@ -347,8 +358,6 @@ def tile_list_phonon_mode_weave_kernel(
                 nc.sync.dma_start(out_rows[:, m0 : m0 + groups, chunk_cols[c]], res[:])
                 next_bank = next_bank + 1
 
-        gain_late = keep.tile([P, 1], F32, name="gain_late", tag="z0", align_bytes=64)
-        nc.gpsimd.tensor_copy(gain_late[:], gain_pool[:])
         for c in PAIR:
             last_slot_on_vector(c, gain_late)
         for c in PAIR:

@@ -33,6 +33,7 @@ BANK_COPIES = 16
 WIDTHS = (256, 256, 512, 512, 512)
 SCALAR_CHUNK = 2
 PAIR = (3, 4)
+POOL_CHUNK = 4
 
 
 def tile_list_phonon_mode_weave_kernel(
@@ -260,13 +261,8 @@ def tile_list_phonon_mode_weave_kernel(
             nc.scalar.copy(t[:], gain_t[:, i : i + 1])
             return t
 
-        def gain_on_gpsimd(i):
-            t = keep.tile([P, 1], F32, name="gain_pool", tag="h2_last")
-            nc.gpsimd.tensor_copy(t[:], gain_t[:, i : i + 1])
-            return t
-
         def slot_on_scalar(c, i, gain_col):
-            nc.scalar.activation(z[c][:, :, i], pages[i][:, chunk_cols[c]], ACT.Copy, scale=gain_col[:])
+            nc.scalar.activation(z[c][:, :, i], pages[i][:, chunk_cols[c]], ACT.Copy, scale=gain_col)
 
         def last_slot_on_vector(c, gain_col):
             nc.vector.tensor_scalar_mul(z[c][:, :, LAST], pages[LAST][:, chunk_cols[c]], gain_col[:])
@@ -297,15 +293,20 @@ def tile_list_phonon_mode_weave_kernel(
             if i < LAST:
                 gain_col = gain_on_scalar(i)
                 for c in range(len(WIDTHS)):
-                    if i < LAST - 1 or c not in PAIR:
-                        slot_on_scalar(c, i, gain_col)
+                    if c == SCALAR_CHUNK:
+                        continue
+                    if c != POOL_CHUNK:
+                        slot_on_scalar(c, i, gain_col[:])
+                slot_on_scalar(SCALAR_CHUNK, i, gain_t[:, i : i + 1])
 
-        gain_pool = gain_on_gpsimd(LAST - 1)
-        for c in PAIR:
+        gain_pool = keep.tile([P, LAST], F32, name="gain_pool", tag="h2_last")
+        nc.gpsimd.tensor_copy(gain_pool[:], gain_t[:, 0:LAST])
+        for i in range(LAST):
             nc.gpsimd.tensor_scalar(
-                z[c][:, :, LAST - 1], pages[LAST - 1][:, chunk_cols[c]], gain_pool[:], 0.0, MULT, ADD
+                z[POOL_CHUNK][:, :, i], pages[i][:, chunk_cols[POOL_CHUNK]], gain_pool[:, i : i + 1], 0.0, MULT, ADD
             )
-        gain_pool = gain_on_gpsimd(LAST)
+        gain_pool = keep.tile([P, 1], F32, name="gain_pool", tag="h2_last")
+        nc.gpsimd.tensor_copy(gain_pool[:], gain_t[:, LAST : LAST + 1])
         gain_col = gain_on_scalar(LAST)
 
         z_w = keep.tile([P, T], U32, name="z_w", align_bytes=64)

from contextlib import ExitStack

import concourse.mybir as mybir

K, K2, H, N, T, S = 512, 1024, 512, 512, 2048, 1024
FLOPS = 2 * K * 2 * H * S + 2 * K2 * H * S + 2 * H * N * T

F32 = mybir.dt.float32
BF16 = mybir.dt.bfloat16
I32 = mybir.dt.int32
U32 = mybir.dt.uint32
U16 = mybir.dt.uint16
U8 = mybir.dt.uint8
FP8X4 = mybir.dt.float8_e4m3fn_x4
FP4X4 = mybir.dt.float4_e2m1fn_x4
ACT = mybir.ActivationFunctionType
MULT = mybir.AluOpType.mult
ADD = mybir.AluOpType.add
EQUAL = mybir.AluOpType.is_equal

P = 128
PACK = 4
LAST = PACK - 1
K_PASS = P * PACK
QUAD = 32
QUADS = (0, 2, 1, 3)
BANK = 512
BANKS = 8
LANES = 16
HALF = S // 2
FIRST = S // 4
BANK_COPIES = 16
WIDTHS = (256, 256, 512, 512, 512)
SCALAR_CHUNK = 2
PAIR = (3, 4)
POOL_CHUNK = 4


def tile_list_phonon_mode_weave_kernel(
    tc, tab_words, tab_scales, tab2_words, tab2_scales, wri_words, wri_scales, w3, w4_words, w4_scales,
    floor, scl, gain, wg1, wg2, offs, offs2, offs3, offs4, out,
):
    nc = tc.nc
    with ExitStack() as ctx:
        lists = ctx.enter_context(tc.tile_pool(name="lists", bufs=1))
        keep = ctx.enter_context(tc.tile_pool(name="keep", bufs=1))
        psum = ctx.enter_context(tc.psum_pool(name="psum", bufs=1))

        def bank(b):
            return psum.tile([P, BANK], F32, name="bank%d" % b)

        def entries(list_tile, j0, j1):
            return list_tile[:, j0 // LANES : j1 // LANES]

        def load_list(src, name):
            t = lists.tile([P, S // LANES], U16, name=name)
            nc.sync.dma_start(t[:], src)
            return t

        def zeroed_plane(width, name):
            t = keep.tile([P, width], U8, name=name, align_bytes=64)
            nc.vector.memset(t[:].bitcast(I32), 0)
            return t

        def load_scales(plane, src):
            for r in range(4):
                nc.sync.dma_start(plane[:].bitcast(I32)[r:P:QUAD, :], src[0, r:16:4, :].bitcast(I32))

        def load_scales_two_passes(plane, src):
            for q in QUADS:
                nc.sync.dma_start(
                    plane[:].bitcast(I32)[QUAD * q : QUAD * q + 8, :], src[:, 4 * q : 4 * q + 4, :].bitcast(I32)
                )

        def load_words(src, width, name):
            t = keep.tile([P, width], I32, name=name, align_bytes=64)
            nc.sync.dma_start(t[:], src.rearrange("p t i -> p (t i)").bitcast(I32))
            return t

        def load_wg(t, src, i, j0, j1):
            rows = src.rearrange("(q i) j -> q (i j)", i=PACK)[:, S * i + j0 : S * i + j1]
            for q in QUADS:
                nc.sync.dma_start(t[QUAD * q : QUAD * (q + 1), S * i + j0 : S * i + j1], rows)

        def load_w3(a):
            t = keep.tile([P, PACK, H], F32, name="w3_raw%d" % a)
            nc.sync.dma_start(t[:], w3[K_PASS * a : K_PASS * (a + 1), :].rearrange("(p j) c -> p j c", j=PACK))
            return t

        def load_channel_vector(src, name):
            t = keep.tile([P, PACK], F32, name=name)
            nc.sync.dma_start(t[:], src.rearrange("(p i) -> p i", i=PACK))
            return t

        tab_plane = keep.tile([P, T], U8, name="tab_plane", align_bytes=64)
        nc.vector.memset(tab_plane[:, 0 : T // 2].bitcast(I32), 0)
        nc.gpsimd.memset(tab_plane[:, T // 2 : T].bitcast(I32), 0)
        wri_plane = zeroed_plane(2 * H, "wri_plane")
        tab2_plane = zeroed_plane(T, "tab2_plane")
        w4_plane = zeroed_plane(N, "w4_plane")
        ident = keep.tile([P, P], F32, name="ident")
        nc.gpsimd.memset(ident[:], 0.0)
        ones = keep.tile([P, QUAD], F32, name="ones")
        nc.vector.memset(ones[:], 1.0)
        count = keep.tile([P, QUAD], F32, name="count", align_bytes=64)
        nc.vector.tensor_tensor_scan(count[:], ones[:], ones[:], 0.0, MULT, ADD)
        turned = keep.tile([P, QUAD], F32, name="turned", align_bytes=64)
        nc.vector.transpose(turned[:], count[:])
        diagonal = keep.tile([P, QUAD], F32, name="diagonal")
        nc.vector.tensor_tensor(diagonal[:], count[:], turned[:], EQUAL)
        for q in range(P // QUAD):
            rows = slice(QUAD * q, QUAD * (q + 1))
            nc.scalar.copy(ident[rows, rows], diagonal[rows, :])

        list1 = load_list(offs, "list1")
        list2 = load_list(offs2, "list2")
        load_scales(tab_plane, tab_scales)
        tab_w = load_words(tab_words[0], T, "tab_w")
        load_scales(wri_plane, wri_scales)
        wri_w = keep.tile([P, 4 * H], U8, name="wri_w", align_bytes=64)
        nc.sync.dma_start(wri_w[:].bitcast(I32), wri_words[0].bitcast(I32))
        load_scales_two_passes(tab2_plane, tab2_scales)
        floor_t = load_channel_vector(floor, "floor_t")
        tab2_w = [load_words(tab2_words[0], T, "tab2_w0")]
        list3 = load_list(offs3, "list3")
        wg1_t = keep.tile([P, PACK * S], F32, name="wg1_t")
        wg2_t = keep.tile([P, PACK * S], F32, name="wg2_t")
        first_rows = wg1.rearrange("(q i) j -> q i j", i=PACK)[:, 0:2, 0:FIRST]
        for q in QUADS:
            by_page = wg1_t[:].rearrange("p (i j) -> p i j", i=PACK)
            nc.sync.dma_start(by_page[QUAD * q : QUAD * (q + 1), 0:2, 0:FIRST], first_rows)
        tab2_w.append(load_words(tab2_words[1], T, "tab2_w1"))
        for i in (2, 3):
            load_wg(wg1_t, wg1, i, 0, HALF)
        w3_raw = []
        for i in (0, 1):
            w3_raw.append(load_w3(i))
            load_wg(wg1_t, wg1, i, FIRST, S)
        for i in (2, 3):
            load_wg(wg1_t, wg1, i, HALF, S)
        list4 = load_list(offs4, "list4")
        gain_t = load_channel_vector(gain, "gain_t")
        scl_t = []
        for i in range(PACK):
            t = keep.tile([P, S], F32, name="scl", tag="wide_row%d" % i)
            nc.sync.dma_start(t[:], scl.rearrange("(p i) j -> p i j", i=PACK)[:, i, :])
            scl_t.append(t)
            load_wg(wg2_t, wg2, i, 0, S)
        w4_w = load_words(w4_words[0], N, "w4_w")
        load_scales(w4_plane, w4_scales)

        warm = keep.tile([P, 1], F32, name="warm")
        nc.scalar.activation(warm[:], ones[:, 0:1], ACT.Sqrt)

        v_scale = keep.tile([P, S], U8, name="v_scale", align_bytes=64)
        nc.vector.tensor_copy(v_scale[:], tab_plane[:].indirect(list1[:]))
        v_w = []
        for j0, j1 in ((0, FIRST), (FIRST, S)):
            t = keep.tile([P, j1 - j0], U32, name="v_w%d" % j0, align_bytes=64)
            nc.vector.tensor_copy(t[:], tab_w[:].bitcast(U32).indirect(entries(list1, j0, j1)))
            v_w.extend(t[:, c : c + P] for c in range(0, j1 - j0, P))
        v2_w = [keep.tile([P, S], U32, name="v2_w%d" % a, align_bytes=64) for a in range(2)]
        v2_scale = keep.tile([P, S], U8, name="v2_scale", align_bytes=64)
        nc.vector.tensor_copy(v2_scale[:], tab2_plane[:].indirect(list2[:]))
        for a in range(2):
            nc.vector.tensor_copy(v2_w[a][:], tab2_w[a][:].bitcast(U32).indirect(list2[:]))

        pages = [keep.tile([P, T], F32, name="page%d" % i) for i in range(PACK)]

        squares = {}

        def project(j0, j1):
            for jb in range(j0 // P, j1 // P):
                for part in range(2):
                    acc = bank(2 * (jb - j0 // P) + part)
                    nc.tensor.matmul_mx(
                        out=acc[:],
                        lhsT=v_w[jb].bitcast(FP8X4),
                        lhsT_scale=v_scale[:, P * jb : P * (jb + 1)],
                        rhs=wri_w[:, 2 * H * part : 2 * H * (part + 1)].bitcast(FP4X4),
                        rhs_scale=wri_plane[:, H * part : H * (part + 1)],
                        start=True,
                        stop=True,
                    )
                    sq = keep.tile([P, PACK, P], F32, name="sq", tag="bank_copy", bufs=BANK_COPIES)
                    nc.scalar.activation(sq[:], acc[:].rearrange("j (p i) -> j i p", i=PACK), ACT.Square)
                    squares[(jb, part)] = sq

        def magnitudes(i, j0, j1, first_bank):
            h1 = keep.tile([P, j1 - j0], F32, name="h1_%d_%d" % (i, j0), align_bytes=64)
            cuts = (j0, HALF, j1) if j0 < HALF < j1 else (j0, j1)
            for n, (c0, c1) in enumerate(zip(cuts, cuts[1:])):
                acc = bank(first_bank + n)
                for jb in range(c0 // P, c1 // P):
                    for part in range(2):
                        nc.tensor.matmul(
                            acc[:, P * jb - c0 : P * (jb + 1) - c0], squares[(jb, part)][:, i, :], ident[:],
                            start=(part == 0), stop=(part == 1), is_transpose=True,
                        )
                nc.scalar.activation(
                    h1[:, c0 - j0 : c1 - j0], acc[:, 0 : c1 - c0], ACT.Sqrt, bias=floor_t[:, i : i + 1]
                )
            return h1

        def stream1_fused(i, j0, j1, first_bank):
            h1 = magnitudes(i, j0, j1, first_bank)
            nc.vector.tensor_tensor(
                pages[i][:].indirect(entries(list3, j0, j1)), h1[:], wg1_t[:, S * i + j0 : S * i + j1], MULT
            )

        def weigh(i, j0, j1, first_bank, weighted=None):
            h1 = magnitudes(i, j0, j1, first_bank)
            weighted = h1 if weighted is None else weighted
            nc.gpsimd.tensor_tensor(weighted[:], h1[:], wg1_t[:, S * i + j0 : S * i + j1], MULT)
            return weighted

        def scatter1(i, j0, j1, weighted):
            nc.vector.tensor_copy(pages[i][:].indirect(entries(list3, j0, j1)), weighted[:])

        def stream1(i, j0, j1, first_bank, weighted=None):
            scatter1(i, j0, j1, weigh(i, j0, j1, first_bank, weighted))

        project(0, FIRST)
        stream1_fused(0, 0, FIRST, 4)
        stream1_fused(1, 0, FIRST, 5)
        project(FIRST, HALF)
        after_fused = keep.tile([P, HALF], F32, name="after_fused", tag="h1_1_0", align_bytes=64)
        stream1(2, 0, HALF, 6, after_fused)
        stream1(3, 0, HALF, 7)
        project(HALF, S)
        stream1(0, FIRST, S, 0)
        weighted1 = keep.tile([P, S - FIRST], F32, name="weighted1")
        weigh(1, FIRST, S, 2, weighted1)

        grouped = keep.tile([P, 2, PACK * H], BF16, name="w3_bf16", align_bytes=64)
        for a in range(2):
            nc.scalar.copy(
                grouped[:, a, :].rearrange("p (i m j) -> p m i j", i=PACK, j=PACK),
                w3_raw[a][:].rearrange("p j (m i) -> p m i j", i=PACK),
            )
        w3_w = keep.tile([P, 2 * H], U32, name="w3_w", tag="h1_1_%d" % FIRST, align_bytes=64)
        w3_plane = keep.tile([P, 2 * H], U8, name="w3_plane", align_bytes=64)
        nc.vector.quantize_mx(
            out=w3_w[:].bitcast(FP8X4), scales=w3_plane[:], in_=grouped[:].rearrange("p a c -> p (a c)")
        )

        scatter1(1, FIRST, S, weighted1)
        after_w3 = keep.tile([P, HALF], F32, name="after_w3", tag="w3_bf16", align_bytes=64)
        stream1(2, HALF, S, 4, after_w3)
        stream1(3, HALF, S, 5)

        starts = [sum(WIDTHS[:c]) for c in range(len(WIDTHS))]
        chunk_cols = [slice(starts[c], starts[c] + WIDTHS[c]) for c in range(len(WIDTHS))]
        z = [
            keep.tile([P, width, PACK], BF16, name="z", tag="z%d" % c, align_bytes=64)
            for c, width in enumerate(WIDTHS)
        ]

        def gain_on_scalar(i):
            t = keep.tile([P, 1], F32, name="gain_col")
            nc.scalar.copy(t[:], gain_t[:, i : i + 1])
            return t

        def slot_on_scalar(c, i, gain_col):
            nc.scalar.activation(z[c][:, :, i], pages[i][:, chunk_cols[c]], ACT.Copy, scale=gain_col)

        def last_slot_on_vector(c, gain_col):
            nc.vector.tensor_scalar_mul(z[c][:, :, LAST], pages[LAST][:, chunk_cols[c]], gain_col[:])

        first_h2_bank = 6
        for i in range(PACK):
            nc.gpsimd.tensor_tensor(scl_t[i][:], scl_t[i][:], wg2_t[:, S * i : S * (i + 1)], MULT)
            for h in range(2):
                acc = bank((first_h2_bank + 2 * i + h) % BANKS)
                cols = slice(HALF * h, HALF * (h + 1))
                for a in range(2):
                    nc.tensor.matmul_mx(
                        out=acc[:],
                        lhsT=w3_w[:, H * a + P * i : H * a + P * (i + 1)].bitcast(FP8X4),
                        lhsT_scale=w3_plane[:, H * a + P * i : H * a + P * (i + 1)],
                        rhs=v2_w[a][:, cols].bitcast(FP8X4),
                        rhs_scale=v2_scale[4 * a : P, cols],
                        start=(a == 0),
                        stop=(a == 1),
                    )
                if i == LAST and h == 1:
                    h2 = keep.tile([P, BANK], F32, name="h2_last")
                else:
                    h2 = keep.tile([P, BANK], F32, name="h2", tag="bank_copy", bufs=BANK_COPIES)
                nc.scalar.copy(h2[:], acc[:])
                nc.gpsimd.tensor_tensor(scl_t[i][:, cols], scl_t[i][:, cols], h2[:], MULT)
            nc.vector.tensor_copy(pages[i][:].indirect(list4[:]), scl_t[i][:])
            if i < LAST:
                gain_col = gain_on_scalar(i)
                for c in range(len(WIDTHS)):
                    if c == SCALAR_CHUNK:
                        continue
                    if c != POOL_CHUNK:
                        slot_on_scalar(c, i, gain_col[:])
                slot_on_scalar(SCALAR_CHUNK, i, gain_t[:, i : i + 1])

        gain_pool = keep.tile([P, LAST], F32, name="gain_pool", tag="h2_last")
        nc.gpsimd.tensor_copy(gain_pool[:], gain_t[:, 0:LAST])
        for i in range(LAST):
            nc.gpsimd.tensor_scalar(
                z[POOL_CHUNK][:, :, i], pages[i][:, chunk_cols[POOL_CHUNK]], gain_pool[:, i : i + 1], 0.0, MULT, ADD
            )
        gain_pool = keep.tile([P, 1], F32, name="gain_pool", tag="h2_last")
        nc.gpsimd.tensor_copy(gain_pool[:], gain_t[:, LAST : LAST + 1])
        gain_col = gain_on_scalar(LAST)

        z_w = keep.tile([P, T], U32, name="z_w", align_bytes=64)
        z_plane = keep.tile([P, T], U8, name="z_plane", align_bytes=64)
        out_rows = out.rearrange("(m p) t -> p m t", p=P)

        def quantise(c):
            cols = chunk_cols[c]
            nc.vector.quantize_mx(
                out=z_w[:, cols].bitcast(FP8X4), scales=z_plane[:, cols], in_=z[c][:].rearrange("p t i -> p (t i)")
            )

        def product(acc, m, c):
            cols = chunk_cols[c]
            nc.tensor.matmul_mx(
                out=acc,
                lhsT=w4_w[:, P * m : P * (m + 1)].bitcast(FP8X4),
                lhsT_scale=w4_plane[:, P * m : P * (m + 1)],
                rhs=z_w[:, cols].bitcast(FP8X4),
                rhs_scale=z_plane[:, cols],
                start=True,
                stop=True,
            )

        gain_first = keep.tile([P, 1], F32, name="gain_first")
        nc.scalar.copy(gain_first[:], gain_t[:, LAST : LAST + 1])
        first = starts[SCALAR_CHUNK]
        gain_late = None
        for c0, c1 in ((0, P), (P, 2 * P), (2 * P, WIDTHS[SCALAR_CHUNK])):
            if c0 == 2 * P:
                gain_late = keep.tile([P, 1], F32, name="gain_late", tag="gain_first")
                nc.scalar.copy(gain_late[:], gain_pool[:])
            nc.scalar.activation(
                z[SCALAR_CHUNK][:, c0:c1, LAST], pages[LAST][:, first + c0 : first + c1], ACT.Copy,
                scale=gain_col[:] if c0 else gain_first[:],
            )
        next_bank = 0
        for c in range(PAIR[0]):
            width = WIDTHS[c]
            if c != SCALAR_CHUNK:
                last_slot_on_vector(c, gain_col)
            quantise(c)
            groups = 1 if c == 0 else BANK // width
            for m0 in range(0, N // P, groups):
                acc = bank(next_bank % BANKS)
                for g in range(groups):
                    product(acc[:, width * g : width * (g + 1)], m0 + g, c)
                res = keep.tile([P, groups, width], F32, name="res", tag="bank_copy", bufs=BANK_COPIES)
                nc.scalar.copy(res[:].rearrange("p g t -> p (g t)"), acc[:, 0 : groups * width])
                nc.sync.dma_start(out_rows[:, m0 : m0 + groups, chunk_cols[c]], res[:])
                next_bank = next_bank + 1

        for c in PAIR:
            last_slot_on_vector(c, gain_late)
        for c in PAIR:
            quantise(c)
        for m in range(N // P):
            res = keep.tile([P, 2 * BANK], F32, name="res_pair", tag="wide_row%d" % m)
            left = bank((next_bank + 2 * m) % BANKS)
            product(left[:], m, PAIR[0])
            nc.vector.tensor_copy(res[:, 0:BANK], left[:])
            right = bank((next_bank + 2 * m + 1) % BANKS)
            product(right[:], m, PAIR[1])
            if m == 0:
                nc.sync.dma_start(out_rows[:, m, chunk_cols[PAIR[0]]], res[:, 0:BANK])
                nc.vector.tensor_copy(res[:, BANK : 2 * BANK], right[:])
                nc.sync.dma_start(out_rows[:, m, chunk_cols[PAIR[1]]], res[:, BANK : 2 * BANK])
            else:
                nc.scalar.copy(res[:, BANK : 2 * BANK], right[:])
                nc.sync.dma_start(out_rows[:, m, starts[PAIR[0]] : T], res[:])
